import numpy as np
import ml_dtypes


def mxq(x, axis, fmt="e4m3"):
    dtype, down = {"e4m3": (ml_dtypes.float8_e4m3fn, 7), "e5m2": (ml_dtypes.float8_e5m2, 14)}[fmt]
    v = np.moveaxis(np.asarray(x, np.float32).astype(ml_dtypes.bfloat16).astype(np.float64), axis, -1)
    blocks = v.reshape(v.shape[:-1] + (-1, 32))
    amax = np.abs(blocks).max(-1, keepdims=True)
    byte = np.maximum(np.where(amax > 0, np.frexp(amax)[1] - 1 + 127, 0) - down, 1)
    scale = np.exp2(byte - 127.0)
    codes = (blocks / scale).astype(np.float32).astype(dtype).astype(np.float64)
    return np.moveaxis((codes * scale).reshape(v.shape), -1, axis)


WIDE = False


def mx_kscale(k):
    if not WIDE:
        return np.ones(k)
    levels = np.array([10, -10, 5, -5, 0])
    if k % 512:
        return np.exp2(np.random.permutation(np.resize(levels, k // 32))).repeat(32)
    a = np.empty((k // 512, 16))
    for p in range(k // 512):
        a[p, :8] = np.random.permutation(np.resize(levels, 8))
        for g in range(8):
            far = levels[np.abs(levels - a[p, g]) >= 10]
            a[p, g + 8] = far[np.random.randint(len(far))]
    return np.exp2(a.ravel()).repeat(32)


BF16 = ml_dtypes.bfloat16


def bf(x):
    return np.asarray(x, np.float32).astype(BF16)


def f64(x):
    return np.asarray(x).astype(np.float64)


E2M1 = np.array([0.0, 0.5, 1.0, 1.5, 2.0, 3.0, 4.0, 6.0, -0.0, -0.5, -1.0, -1.5, -2.0, -3.0, -4.0, -6.0])


def pack_weight(w, fmt):
    k, n = w.shape
    w = f64(bf(w)).reshape(k // 32, 32, n)
    amax = np.abs(w).max(1)
    if fmt == "e4m3":
        byte = np.frexp(amax)[1] - 1 + 127 - 7
    else:
        mant, ex = np.frexp(amax / 6.0)
        byte = np.where(mant > 0.5, ex, ex - 1) + 127
    byte = np.clip(np.where(amax > 0, byte, 1), 1, 254)
    scaled = (w * np.exp2(127.0 - byte)[:, None, :]).reshape(k, n).astype(np.float32)
    by_word = np.ascontiguousarray(scaled.reshape(k // 512, 128, 4, n).transpose(0, 1, 3, 2))
    if fmt == "e4m3":
        words = by_word.astype(ml_dtypes.float8_e4m3fn).view(np.uint8)
    else:
        c = by_word.astype(ml_dtypes.float4_e2m1fn).view(np.uint8) & 0xF
        words = c[..., 0::2] | (c[..., 1::2] << 4)
    return np.ascontiguousarray(words), np.ascontiguousarray(byte.astype(np.uint8).reshape(k // 512, 16, n))


def unpack_weight(words, scales, fmt):
    g, p, n, _ = words.shape
    if fmt == "e4m3":
        vals = np.ascontiguousarray(words).view(ml_dtypes.float8_e4m3fn).astype(np.float64)
    else:
        nib = np.empty((g, p, n, 4), np.uint8)
        nib[..., 0::2] = words & 0xF
        nib[..., 1::2] = words >> 4
        vals = E2M1[nib]
    vals = vals * np.repeat(np.exp2(scales.astype(np.float64) - 127.0), 8, axis=1)[..., None]
    return vals.transpose(0, 1, 3, 2).reshape(g * 512, n)
def pack4(w):
    words, scales = pack_weight(w, "e2m1")
    return words.reshape(words.shape[0], 128, -1), scales


def unpack4(words, scales):
    return unpack_weight(words.reshape(words.shape[0], 128, -1, 2), scales, "e2m1")


Q, H, V, D, L = 512, 1024, 3072, 1024, 512


def setup_inputs():
    s, r, t = mx_kscale(H), mx_kscale(L), mx_kscale(V)
    E = 2.0 * np.random.standard_normal((H, V)) / np.sqrt(H) / s[:, None]
    e_words, e_scales = pack4(E)
    return {"xq": bf(np.random.standard_normal((Q, H)) * s),
            "e_words": e_words,
            "e_scales": e_scales,
            "idf": bf(2.0 * (1 + 0.1 * np.random.standard_normal(V)) / V ** 0.25 * t),
            "xd": bf(np.random.standard_normal((D, L)) * r),
            "w": bf(np.random.standard_normal((L, V)) / np.sqrt(L) / V ** 0.25 / r[:, None] / t)}


def reference(xq, e_words, e_scales, idf, xd, w):
    z = mxq(f64(xq), 1, "e4m3") @ unpack4(e_words, e_scales)
    u = np.log(1.0 + np.maximum(z, 0.0)) * f64(idf)
    d = mxq(f64(xd), 1, "e4m3") @ mxq(f64(w), 0, "e4m3")
    return mxq(u, 1, "e4m3") @ mxq(d, 1, "e4m3").T

@@ -1,0 +1,389 @@
+from contextlib import ExitStack
+
+import concourse.mybir as mybir
+from concourse.masks import make_identity
+
+Q, H, V, D, L = 512, 1024, 3072, 1024, 512
+FLOPS = 2 * Q * H * V + 2 * D * L * V + 2 * Q * V * D
+
+F32 = mybir.dt.float32
+BF16 = mybir.dt.bfloat16
+I32 = mybir.dt.int32
+U32 = mybir.dt.uint32
+U8 = mybir.dt.uint8
+FP8X4 = mybir.dt.float8_e4m3fn_x4
+FP4X4 = mybir.dt.float4_e2m1fn_x4
+ALU = mybir.AluOpType
+ACT = mybir.ActivationFunctionType
+
+P = 128
+PACK = 4
+K_PASS = P * PACK
+GROUPS = V // K_PASS
+H_PASSES = H // K_PASS
+Q_TILES = Q // P
+HALF = 512
+HALVES = D // HALF
+DOC_TILES = HALF // P
+RUN = 8
+BLOCKS = P // RUN
+
+
+def tile_log_saturated_latent_scoring_s11_kernel(tc, xq, e_words, e_scales, idf, xd, w, out):
+    nc = tc.nc
+    with ExitStack() as ctx:
+        keep = ctx.enter_context(tc.tile_pool(name="keep", bufs=1))
+        stage = ctx.enter_context(tc.tile_pool(name="stage", bufs=2))
+        fill = ctx.enter_context(tc.psum_pool(name="fill", bufs=1))
+        sums = ctx.enter_context(tc.psum_pool(name="sums", bufs=4))
+        ctx.enter_context(tc.manual_schedule())
+
+        def kept(name, shape, dtype):
+            return keep.tile(shape, dtype, name=name, align_bytes=64)
+
+        def staged(tag, shape, dtype, bufs):
+            return stage.tile(shape, dtype, name=tag, tag=tag, bufs=bufs, align_bytes=64)
+
+        taken = {True: 0, False: 0}
+        banks = {True: (3,), False: (0, 1, 2)}
+
+        def new_bank(on_vector):
+            mine = banks[on_vector]
+            tag = "bank%d" % mine[taken[on_vector] % len(mine)]
+            taken[on_vector] = taken[on_vector] + 1
+            return fill.tile([P, PACK, P], F32, name=tag, tag=tag)
+
+        def copy_out(on_vector, dst, src):
+            if on_vector:
+                nc.vector.tensor_copy(out=dst, in_=src)
+            else:
+                nc.scalar.copy(out=dst, in_=src)
+
+        def quantize(codes, scales, values):
+            nc.vector.quantize_mx(out=codes.bitcast(FP8X4), scales=scales, in_=values)
+
+        ident = kept("ident", [P, P], F32)
+        make_identity(nc, ident[:])
+        idf_rows = kept("idf_rows", [P, K_PASS], F32)
+        nc.gpsimd.memset(idf_rows[:], 0.0)
+        es_raw = kept("es_raw", [P, H_PASSES, V], U8)
+        nc.vector.memset(es_raw[:].bitcast(I32), 0)
+
+        xd_raw, w_raw, xq_raw, ew_raw = {}, {}, {}, {}
+
+        def load_xd(part):
+            xd_raw[part] = kept("xd_raw%d" % part, [P, 2 * L], BF16)
+            nc.sync.dma_start(out=xd_raw[part][:], in_=xd[part * 256 : (part + 1) * 256, :].rearrange("(p a) k -> p (a k)", a=2))
+
+        def load_w(g):
+            w_raw[g] = kept("w_raw%d" % g, [P, PACK, K_PASS], BF16)
+            nc.sync.dma_start(out=w_raw[g][:], in_=w[:, g * K_PASS : (g + 1) * K_PASS].rearrange("(p j) v -> p j v", j=PACK))
+
+        def load_xq(pair):
+            xq_raw[pair] = kept("xq_raw%d" % pair, [P, 2, H], BF16)
+            nc.sync.dma_start(out=xq_raw[pair][:], in_=xq[pair * 2 * P : (pair + 1) * 2 * P, :].rearrange("(i p) k -> p i k", i=2))
+
+        def load_e_words(pair):
+            ew_raw[pair] = kept("ew_raw%d" % pair, [P, H_PASSES, K_PASS], I32)
+            nc.sync.dma_start(
+                out=ew_raw[pair][:],
+                in_=e_words.bitcast(I32)[:, :, pair * K_PASS : (pair + 1) * K_PASS].rearrange("c p n -> p c n"),
+            )
+
+        idf_raw = kept("idf_raw", [GROUPS, K_PASS], BF16)
+
+        nc.scalar.dma_start(out=idf_raw[:], in_=idf.rearrange("(g v) -> g v", g=GROUPS))
+        warm = kept("warm", [P, 1], F32)
+        nc.scalar.activation(out=warm[:], in_=ident[:, 0:1], func=ACT.Ln, bias=1.0)
+        load_xd(0)
+        load_w(0)
+        load_xd(1)
+        load_xd(2)
+        load_xd(3)
+        load_w(1)
+        load_xq(0)
+        for quad in range(4):
+            nc.sync.dma_start(
+                out=es_raw[32 * quad : 32 * quad + 4, :, :].bitcast(I32),
+                in_=e_scales.bitcast(I32)[:, 4 * quad : 4 * quad + 4, :].rearrange("c r n -> r c n"),
+            )
+        load_e_words(0)
+        load_w(2)
+        load_e_words(1)
+        load_w(3)
+        load_w(4)
+        load_e_words(2)
+        load_w(5)
+        load_xq(1)
+
+        xd_t = [kept("xd_t%d" % h, [P, HALF, PACK], BF16) for h in range(HALVES)]
+        xd_codes = [kept("xd_codes%d" % h, [P, HALF], U32) for h in range(HALVES)]
+        xd_scales = [kept("xd_scales%d" % h, [P, HALF], U8) for h in range(HALVES)]
+
+        def turn_xd(h, n, on_vector):
+            words = xd_raw[2 * h + n][:].bitcast(F32)
+            bank = new_bank(on_vector)
+            for a in range(2):
+                for u in range(2):
+                    nc.tensor.transpose(bank[:, 2 * a + u, :], words[:, 256 * a + u : 256 * (a + 1) : 2], ident[:])
+            dst = xd_t[h][:, 256 * n : 256 * (n + 1), :].rearrange("k d t -> k (d t)").bitcast(F32)
+            copy_out(on_vector, dst.rearrange("k (p j) -> k p j", j=PACK), bank[:].rearrange("k j p -> k p j"))
+
+        def quantize_xd(h, d0, d1):
+            quantize(xd_codes[h][:, d0:d1], xd_scales[h][:, d0:d1], xd_t[h][:, d0:d1, :].rearrange("k d t -> k (d t)"))
+
+        xq_t = [kept("xq_t%d" % i, [P, H_PASSES * P * PACK], BF16) for i in range(Q_TILES)]
+        xq_codes = [kept("xq_codes%d" % i, [P, H_PASSES * P], U32) for i in range(Q_TILES)]
+        xq_scales = [kept("xq_scales%d" % i, [P, H_PASSES * P], U8) for i in range(Q_TILES)]
+
+        def turn_xq(i, on_vector):
+            words = xq_raw[i // 2][:].bitcast(F32)
+            bank = new_bank(on_vector)
+            for c in range(H_PASSES):
+                for u in range(2):
+                    nc.tensor.transpose(bank[:, 2 * c + u, :], words[:, i % 2, 256 * c + u : 256 * (c + 1) : 2], ident[:])
+            copy_out(
+                on_vector,
+                xq_t[i][:].bitcast(F32).rearrange("k (c q u) -> k c q u", c=H_PASSES, u=2),
+                bank[:].rearrange("k (c u) q -> k c q u", u=2),
+            )
+
+        def quantize_xq(i):
+            quantize(xq_codes[i][:], xq_scales[i][:], xq_t[i][:])
+
+        idf_cols = kept("idf_cols", [P, GROUPS, PACK], F32)
+
+        def turn_idf():
+            nc.gpsimd.tensor_copy(
+                out=idf_rows[0:GROUPS, :].rearrange("g (t q r) -> g t q r", t=PACK, r=RUN),
+                in_=idf_raw[:].rearrange("g (q t r) -> g t q r", t=PACK, r=RUN),
+            )
+            bank = new_bank(False)
+            for t in range(PACK):
+                nc.tensor.transpose(bank[:, t, :], idf_rows[:, t * P : (t + 1) * P], ident[:])
+            nc.scalar.copy(out=idf_cols[:], in_=bank[:, :, 0:GROUPS].rearrange("m t g -> m g t"))
+
+        es_sorted = kept("es_sorted", [P, H_PASSES * GROUPS, K_PASS], U8)
+        ew_sorted = [kept("ew_sorted%d" % pair, [P, H_PASSES * 2, 2 * K_PASS], U8) for pair in range(GROUPS // 2)]
+
+        def sort_e_scales():
+            nc.vector.tensor_copy(
+                out=es_sorted[:].bitcast(I32).rearrange("p s (t q r) -> p s t q r", t=PACK, q=BLOCKS),
+                in_=es_raw[:].bitcast(I32).rearrange("p c (g q t r) -> p (c g) t q r", g=GROUPS, t=PACK, q=BLOCKS),
+            )
+
+        def sort_e_words(pair):
+            nc.vector.tensor_copy(
+                out=ew_sorted[pair][:].bitcast(I32).rearrange("p s (t q r) -> p s t q r", t=PACK, q=BLOCKS),
+                in_=ew_raw[pair][:].rearrange("p c (g q t r) -> p (c g) t q r", g=2, t=PACK, q=BLOCKS),
+            )
+
+        w_t, w_codes, w_scales = {}, {}, {}
+
+        def interleave_w(g):
+            w_t[g] = staged("w_t", [P, K_PASS * PACK], BF16, 2)
+            nc.vector.tensor_copy(
+                out=w_t[g][:].rearrange("p (t q r j) -> p t q r j", t=PACK, r=RUN, j=PACK),
+                in_=w_raw[g][:].rearrange("p j (q t r) -> p t q r j", t=PACK, r=RUN),
+            )
+
+        def quantize_w(g):
+            w_codes[g] = staged("w_codes", [P, K_PASS], U32, 2)
+            w_scales[g] = staged("w_scales", [P, K_PASS], U8, 2)
+            quantize(w_codes[g][:], w_scales[g][:], w_t[g][:])
+
+        d_t, d_codes, d_scales = {}, {}, {}
+
+        def make_d(g, doc_tile, on_vector=False):
+            h, n = divmod(doc_tile, DOC_TILES)
+            if n == 0:
+                d_t[g, h] = staged("d_t", [P, HALF, PACK], BF16, 3)
+            docs = slice(n * P, (n + 1) * P)
+            bank = new_bank(on_vector)
+            for t in range(PACK):
+                terms = slice(t * P, (t + 1) * P)
+                nc.tensor.matmul_mx(
+                    out=bank[:, t, :],
+                    lhsT=w_codes[g][:, terms].bitcast(FP8X4), lhsT_scale=w_scales[g][:, terms],
+                    rhs=xd_codes[h][:, docs].bitcast(FP8X4), rhs_scale=xd_scales[h][:, docs],
+                    start=True, stop=True,
+                )
+            copy_out(on_vector, d_t[g, h][:, docs, :], bank[:].rearrange("m t n -> m n t"))
+
+        def quantize_d(g, h):
+            d_codes[g, h] = kept("d_codes%d_%d" % (g, h), [P, HALF], U32)
+            d_scales[g, h] = kept("d_scales%d_%d" % (g, h), [P, HALF], U8)
+            quantize(d_codes[g, h][:], d_scales[g, h][:], d_t[g, h][:].rearrange("m n t -> m (n t)"))
+
+        units = [((g, 0), (g, 1)) for g in range(GROUPS)]
+        units = units + [((g, i), (g + 1, i)) for i in (2, 3) for g in range(0, GROUPS, 2)]
+        z_pos, z_log, u_t, u_codes, u_scales = {}, {}, {}, {}, {}
+
+        def make_z(u, b, on_vector):
+            g, i = units[u][b]
+            if b == 0:
+                z_pos[u] = staged("z_pos", [P, 2, P, PACK], F32, 2)
+            bank = new_bank(on_vector)
+            for t in range(PACK):
+                for c in range(H_PASSES):
+                    qs = slice(c * P, (c + 1) * P)
+                    nc.tensor.matmul_mx(
+                        out=bank[:, t, :],
+                        lhsT=ew_sorted[g // 2][:, 2 * c + g % 2, 2 * P * t : 2 * P * (t + 1)].bitcast(FP4X4),
+                        lhsT_scale=es_sorted[:, GROUPS * c + g, P * t : P * (t + 1)],
+                        rhs=xq_codes[i][:, qs].bitcast(FP8X4), rhs_scale=xq_scales[i][:, qs],
+                        start=(c == 0), stop=(c == H_PASSES - 1),
+                    )
+            z = bank[:].rearrange("m t n -> m n t")
+            if on_vector:
+                nc.vector.tensor_scalar(out=z_pos[u][:, b, :, :], in0=z, scalar1=0.0, scalar2=None, op0=ALU.max)
+            else:
+                nc.scalar.activation(out=z_pos[u][:, b, :, :], in_=z, func=ACT.Relu)
+
+        def log_z(u, b0, b1):
+            if b0 == 0:
+                z_log[u] = staged("z_log", [P, 2, P, PACK], F32, 2)
+            nc.scalar.activation(out=z_log[u][:, b0:b1, :, :], in_=z_pos[u][:, b0:b1, :, :], func=ACT.Ln, bias=1.0)
+
+        def weigh(u, b0, b1):
+            if b0 == 0:
+                u_t[u] = staged("u_t", [P, 2, P, PACK], BF16, 2)
+            g0, g1 = units[u][b0][0], units[u][b1 - 1][0]
+            factors = idf_cols[:, g0 : g1 + 1, :].unsqueeze(2).to_broadcast([P, b1 - b0, P, PACK])
+            nc.vector.tensor_tensor(out=u_t[u][:, b0:b1, :, :], in0=z_log[u][:, b0:b1, :, :], in1=factors, op=ALU.mult)
+
+        def quantize_u(u, b0, b1):
+            if b0 == 0:
+                u_codes[u] = staged("u_codes", [P, 2 * P], U32, 4)
+                u_scales[u] = staged("u_scales", [P, 2 * P], U8, 4)
+            cols = slice(b0 * P, b1 * P)
+            quantize(u_codes[u][:, cols], u_scales[u][:, cols], u_t[u][:, b0:b1, :, :].rearrange("m b n t -> m (b n t)"))
+
+        acc = {}
+
+        def score(u, b):
+            g, i = units[u][b]
+            cols = slice(b * P, (b + 1) * P)
+            for h in range(HALVES):
+                if g == 0:
+                    acc[i, h] = sums.tile([P, HALF], F32, name="acc", tag="acc")
+                nc.tensor.matmul_mx(
+                    out=acc[i, h][:],
+                    lhsT=u_codes[u][:, cols].bitcast(FP8X4), lhsT_scale=u_scales[u][:, cols],
+                    rhs=d_codes[g, h][:].bitcast(FP8X4), rhs_scale=d_scales[g, h][:],
+                    start=(g == 0), stop=(g == GROUPS - 1),
+                )
+
+        def store(i, h, on_vector):
+            result = staged("result", [P, HALF], F32, 4)
+            copy_out(on_vector, result[:], acc[i, h][:])
+            nc.sync.dma_start(out=out[i * P : (i + 1) * P, h * HALF : (h + 1) * HALF], in_=result[:])
+
+        turn_xd(0, 0, False)
+        turn_idf()
+        turn_xd(0, 1, False)
+        interleave_w(0)
+        quantize_xd(0, 0, 256)
+        quantize_w(0)
+        turn_xd(1, 0, False)
+        make_d(0, 0)
+        make_d(0, 1)
+        quantize_xd(0, 256, 512)
+        interleave_w(1)
+        turn_xd(1, 1, True)
+        make_d(0, 2)
+        make_d(0, 3)
+        quantize_w(1)
+        quantize_xd(1, 0, 512)
+        turn_xq(0, True)
+        make_d(0, 4)
+        make_d(0, 5)
+        quantize_d(0, 0)
+        turn_xq(1, True)
+        quantize_xq(0)
+        make_d(0, 6)
+        make_d(0, 7)
+        sort_e_scales()
+        quantize_xq(1)
+        sort_e_words(0)
+
+        for g in range(1, GROUPS):
+            u = g - 1
+            more = g + 1 < GROUPS
+            make_d(g, 0)
+            if more:
+                interleave_w(g + 1)
+            else:
+                turn_xq(2, True)
+            make_d(g, 1)
+            if u >= 1:
+                log_z(u - 1, 0, 2)
+            quantize_d(g - 1, 1)
+            make_d(g, 2)
+            make_d(g, 3)
+            make_z(u, 0, True)
+            make_d(g, 4)
+            if u >= 2:
+                score(u - 2, 0)
+            if more:
+                quantize_w(g + 1)
+            else:
+                quantize_xq(2)
+            make_d(g, 5)
+            if u >= 1:
+                weigh(u - 1, 0, 2)
+            make_z(u, 1, True)
+            make_d(g, 6)
+            quantize_d(g, 0)
+            make_d(g, 7)
+            if u >= 1:
+                quantize_u(u - 1, 0, 2)
+            if u >= 2:
+                score(u - 2, 1)
+            if g in (2, 4):
+                sort_e_words(g // 2)
+
+        banks[True] = (3, 2)
+        banks[False] = (0, 1)
+        last = len(units) - 1
+        first = GROUPS - 1
+        for u in range(first, last + 1):
+            log_z(u - 1, 0, 2)
+            make_z(u, 0, True)
+            if u == first:
+                quantize_d(GROUPS - 1, 1)
+            else:
+                quantize_u(u - 2, 0, 2)
+            make_z(u, 1, False)
+            if u == first:
+                turn_xq(3, False)
+            weigh(u - 1, 0, 2)
+            if u == first + 1:
+                quantize_xq(3)
+            if u > first:
+                score(u - 3, 0)
+                score(u - 3, 1)
+            if u == 8:
+                store(0, 0, False)
+                store(0, 1, True)
+            if u == 9:
+                store(1, 0, False)
+            if u == 10:
+                store(1, 1, False)
+        log_z(last, 0, 1)
+        log_z(last, 1, 2)
+        weigh(last, 0, 1)
+        quantize_u(last - 1, 0, 2)
+        score(last - 2, 0)
+        score(last - 2, 1)
+        store(2, 0, False)
+        weigh(last, 1, 2)
+        score(last - 1, 0)
+        score(last - 1, 1)
+        quantize_u(last, 0, 1)
+        quantize_u(last, 1, 2)
+        store(2, 1, False)
+        score(last, 0)
+        score(last, 1)
+        store(3, 0, False)
+        store(3, 1, True)

@@ -34,8 +34,7 @@ def tile_log_saturated_latent_scoring_s11_kernel(tc, xq, e_words, e_scales, idf,
     with ExitStack() as ctx:
         keep = ctx.enter_context(tc.tile_pool(name="keep", bufs=1))
         stage = ctx.enter_context(tc.tile_pool(name="stage", bufs=2))
-        fill = ctx.enter_context(tc.psum_pool(name="fill", bufs=1))
-        sums = ctx.enter_context(tc.psum_pool(name="sums", bufs=4))
+        psum = ctx.enter_context(tc.psum_pool(name="psum", bufs=1))
         ctx.enter_context(tc.manual_schedule())
 
         def kept(name, shape, dtype):
@@ -44,14 +43,16 @@ def tile_log_saturated_latent_scoring_s11_kernel(tc, xq, e_words, e_scales, idf,
         def staged(tag, shape, dtype, bufs):
             return stage.tile(shape, dtype, name=tag, tag=tag, bufs=bufs, align_bytes=64)
 
-        taken = {True: 0, False: 0}
-        banks = {True: (3,), False: (0, 1, 2)}
+        oldest_first = list(range(8))
+        banks = {True: (3, 4), False: (0, 1, 2, 5, 6)}
 
-        def new_bank(on_vector):
-            mine = banks[on_vector]
-            tag = "bank%d" % mine[taken[on_vector] % len(mine)]
-            taken[on_vector] = taken[on_vector] + 1
-            return fill.tile([P, PACK, P], F32, name=tag, tag=tag)
+        def take_bank(b, shape):
+            oldest_first.remove(b)
+            oldest_first.append(b)
+            return psum.tile(shape, F32, name="bank%d" % b, tag="bank%d" % b)
+
+        def new_bank(on_vector, shape):
+            return take_bank([b for b in oldest_first if b in banks[on_vector]][0], shape)
 
         def copy_out(on_vector, dst, src):
             if on_vector:
@@ -66,8 +67,15 @@ def tile_log_saturated_latent_scoring_s11_kernel(tc, xq, e_words, e_scales, idf,
         make_identity(nc, ident[:])
         idf_rows = kept("idf_rows", [P, K_PASS], F32)
         nc.gpsimd.memset(idf_rows[:], 0.0)
-        es_raw = kept("es_raw", [P, H_PASSES, V], U8)
-        nc.vector.memset(es_raw[:].bitcast(I32), 0)
+        zeros = kept("zeros", [P, P * PACK], BF16)
+        nc.vector.memset(zeros[:], 0.0)
+        zero_codes = kept("zero_codes", [P, P], U32)
+        zero_scales = kept("zero_scales", [P, P], U8)
+        quantize(zero_codes[:], zero_scales[:], zeros[:])
+        es_spans = ((0, 2), (2, GROUPS))
+        es_raw = [kept("es_raw%d" % g0, [P, H_PASSES, (g1 - g0) * K_PASS], U8) for g0, g1 in es_spans]
+        for plane in es_raw:
+            nc.vector.memset(plane[:].bitcast(I32), 0)
 
         xd_raw, w_raw, xq_raw, ew_raw = {}, {}, {}, {}
 
@@ -75,46 +83,62 @@ def tile_log_saturated_latent_scoring_s11_kernel(tc, xq, e_words, e_scales, idf,
             xd_raw[part] = kept("xd_raw%d" % part, [P, 2 * L], BF16)
             nc.sync.dma_start(out=xd_raw[part][:], in_=xd[part * 256 : (part + 1) * 256, :].rearrange("(p a) k -> p (a k)", a=2))
 
-        def load_w(g):
-            w_raw[g] = kept("w_raw%d" % g, [P, PACK, K_PASS], BF16)
-            nc.sync.dma_start(out=w_raw[g][:], in_=w[:, g * K_PASS : (g + 1) * K_PASS].rearrange("(p j) v -> p j v", j=PACK))
+        def load_w(g, part, parts):
+            width = K_PASS // parts
+            w_raw[g, part] = staged("w_raw", [P, PACK, width], BF16, 4)
+            cols = slice(g * K_PASS + part * width, g * K_PASS + (part + 1) * width)
+            nc.sync.dma_start(out=w_raw[g, part][:], in_=w[:, cols].rearrange("(p j) v -> p j v", j=PACK))
 
-        def load_xq(pair):
-            xq_raw[pair] = kept("xq_raw%d" % pair, [P, 2, H], BF16)
-            nc.sync.dma_start(out=xq_raw[pair][:], in_=xq[pair * 2 * P : (pair + 1) * 2 * P, :].rearrange("(i p) k -> p i k", i=2))
+        def load_xq(i):
+            xq_raw[i] = kept("xq_raw%d" % i, [P, H], BF16)
+            nc.sync.dma_start(out=xq_raw[i][:], in_=xq[i * P : (i + 1) * P, :])
 
-        def load_e_words(pair):
-            ew_raw[pair] = kept("ew_raw%d" % pair, [P, H_PASSES, K_PASS], I32)
+        def load_e_words(g):
+            ew_raw[g] = staged("ew_raw", [P, H_PASSES, 256], I32, 4)
             nc.sync.dma_start(
-                out=ew_raw[pair][:],
-                in_=e_words.bitcast(I32)[:, :, pair * K_PASS : (pair + 1) * K_PASS].rearrange("c p n -> p c n"),
+                out=ew_raw[g][:],
+                in_=e_words.bitcast(I32)[:, :, g * 256 : (g + 1) * 256].rearrange("c p n -> p c n"),
             )
 
-        idf_raw = kept("idf_raw", [GROUPS, K_PASS], BF16)
+        def load_e_scales(part):
+            g0, g1 = es_spans[part]
+            for quad in range(4):
+                nc.sync.dma_start(
+                    out=es_raw[part][32 * quad : 32 * quad + 4, :, :].bitcast(I32),
+                    in_=e_scales[:, 4 * quad : 4 * quad + 4, g0 * K_PASS : g1 * K_PASS].bitcast(I32).rearrange("c r n -> r c n"),
+                )
 
+        idf_raw = kept("idf_raw", [GROUPS, K_PASS], BF16)
         nc.scalar.dma_start(out=idf_raw[:], in_=idf.rearrange("(g v) -> g v", g=GROUPS))
         warm = kept("warm", [P, 1], F32)
         nc.scalar.activation(out=warm[:], in_=ident[:, 0:1], func=ACT.Ln, bias=1.0)
+
         load_xd(0)
-        load_w(0)
+        load_w(0, 0, 2)
+        load_w(0, 1, 2)
         load_xd(1)
         load_xd(2)
         load_xd(3)
-        load_w(1)
+        load_w(1, 0, 1)
         load_xq(0)
-        for quad in range(4):
-            nc.sync.dma_start(
-                out=es_raw[32 * quad : 32 * quad + 4, :, :].bitcast(I32),
-                in_=e_scales.bitcast(I32)[:, 4 * quad : 4 * quad + 4, :].rearrange("c r n -> r c n"),
-            )
-        load_e_words(0)
-        load_w(2)
-        load_e_words(1)
-        load_w(3)
-        load_w(4)
-        load_e_words(2)
-        load_w(5)
         load_xq(1)
+        load_xq(2)
+        load_xq(3)
+        load_w(2, 0, 1)
+        load_e_scales(0)
+        load_e_words(0)
+        load_e_words(1)
+        load_e_scales(1)
+
+        def warm_up(passes):
+            bank = take_bank(7, [P, PACK, P])
+            for n in range(passes):
+                nc.tensor.matmul_mx(
+                    out=bank[:, n % PACK, :],
+                    lhsT=zero_codes[:].bitcast(FP8X4), lhsT_scale=zero_scales[:],
+                    rhs=zero_codes[:].bitcast(FP8X4), rhs_scale=zero_scales[:],
+                    start=True, stop=True,
+                )
 
         xd_t = [kept("xd_t%d" % h, [P, HALF, PACK], BF16) for h in range(HALVES)]
         xd_codes = [kept("xd_codes%d" % h, [P, HALF], U32) for h in range(HALVES)]
@@ -122,7 +146,7 @@ def tile_log_saturated_latent_scoring_s11_kernel(tc, xq, e_words, e_scales, idf,
 
         def turn_xd(h, n, on_vector):
             words = xd_raw[2 * h + n][:].bitcast(F32)
-            bank = new_bank(on_vector)
+            bank = new_bank(on_vector, [P, PACK, P])
             for a in range(2):
                 for u in range(2):
                     nc.tensor.transpose(bank[:, 2 * a + u, :], words[:, 256 * a + u : 256 * (a + 1) : 2], ident[:])
@@ -132,60 +156,61 @@ def tile_log_saturated_latent_scoring_s11_kernel(tc, xq, e_words, e_scales, idf,
         def quantize_xd(h, d0, d1):
             quantize(xd_codes[h][:, d0:d1], xd_scales[h][:, d0:d1], xd_t[h][:, d0:d1, :].rearrange("k d t -> k (d t)"))
 
-        xq_t = [kept("xq_t%d" % i, [P, H_PASSES * P * PACK], BF16) for i in range(Q_TILES)]
-        xq_codes = [kept("xq_codes%d" % i, [P, H_PASSES * P], U32) for i in range(Q_TILES)]
-        xq_scales = [kept("xq_scales%d" % i, [P, H_PASSES * P], U8) for i in range(Q_TILES)]
+        xq_t = [kept("xq_t%d" % c, [P, Q * PACK], BF16) for c in range(H_PASSES)]
+        xq_codes = kept("xq_codes", [P, H_PASSES, Q], U32)
+        xq_scales = kept("xq_scales", [P, H_PASSES, Q], U8)
 
-        def turn_xq(i, on_vector):
-            words = xq_raw[i // 2][:].bitcast(F32)
-            bank = new_bank(on_vector)
-            for c in range(H_PASSES):
+        def turn_xq(c, pair, on_vector):
+            bank = new_bank(on_vector, [P, PACK, P])
+            for a in range(2):
+                words = xq_raw[2 * pair + a][:].bitcast(F32)
                 for u in range(2):
-                    nc.tensor.transpose(bank[:, 2 * c + u, :], words[:, i % 2, 256 * c + u : 256 * (c + 1) : 2], ident[:])
-            copy_out(
-                on_vector,
-                xq_t[i][:].bitcast(F32).rearrange("k (c q u) -> k c q u", c=H_PASSES, u=2),
-                bank[:].rearrange("k (c u) q -> k c q u", u=2),
-            )
+                    nc.tensor.transpose(bank[:, 2 * a + u, :], words[:, 256 * c + u : 256 * (c + 1) : 2], ident[:])
+            dst = xq_t[c][:, 1024 * pair : 1024 * (pair + 1)].bitcast(F32)
+            copy_out(on_vector, dst.rearrange("k (a q u) -> k a q u", a=2, u=2), bank[:].rearrange("k (a u) q -> k a q u", u=2))
 
-        def quantize_xq(i):
-            quantize(xq_codes[i][:], xq_scales[i][:], xq_t[i][:])
+        def quantize_xq(c):
+            quantize(xq_codes[:, c, :], xq_scales[:, c, :], xq_t[c][:])
 
         idf_cols = kept("idf_cols", [P, GROUPS, PACK], F32)
 
-        def turn_idf():
-            nc.gpsimd.tensor_copy(
+        def sort_idf():
+            nc.scalar.copy(
                 out=idf_rows[0:GROUPS, :].rearrange("g (t q r) -> g t q r", t=PACK, r=RUN),
                 in_=idf_raw[:].rearrange("g (q t r) -> g t q r", t=PACK, r=RUN),
             )
-            bank = new_bank(False)
+
+        def turn_idf():
+            bank = new_bank(False, [P, PACK, P])
             for t in range(PACK):
                 nc.tensor.transpose(bank[:, t, :], idf_rows[:, t * P : (t + 1) * P], ident[:])
             nc.scalar.copy(out=idf_cols[:], in_=bank[:, :, 0:GROUPS].rearrange("m t g -> m g t"))
 
-        es_sorted = kept("es_sorted", [P, H_PASSES * GROUPS, K_PASS], U8)
-        ew_sorted = [kept("ew_sorted%d" % pair, [P, H_PASSES * 2, 2 * K_PASS], U8) for pair in range(GROUPS // 2)]
+        es_sorted = [kept("es_sorted%d" % g0, [P, H_PASSES, g1 - g0, K_PASS], U8) for g0, g1 in es_spans]
+        ew_sorted = {}
 
-        def sort_e_scales():
+        def sort_e_scales(part):
             nc.vector.tensor_copy(
-                out=es_sorted[:].bitcast(I32).rearrange("p s (t q r) -> p s t q r", t=PACK, q=BLOCKS),
-                in_=es_raw[:].bitcast(I32).rearrange("p c (g q t r) -> p (c g) t q r", g=GROUPS, t=PACK, q=BLOCKS),
+                out=es_sorted[part][:].bitcast(I32).rearrange("p c g (t q r) -> p (c g) t q r", t=PACK, q=BLOCKS),
+                in_=es_raw[part][:].bitcast(I32).rearrange("p c (g q t r) -> p (c g) t q r", t=PACK, q=BLOCKS, r=2),
             )
 
-        def sort_e_words(pair):
+        def sort_e_words(g):
+            ew_sorted[g] = staged("ew_sorted", [P, H_PASSES, 2 * K_PASS], U8, 3)
             nc.vector.tensor_copy(
-                out=ew_sorted[pair][:].bitcast(I32).rearrange("p s (t q r) -> p s t q r", t=PACK, q=BLOCKS),
-                in_=ew_raw[pair][:].rearrange("p c (g q t r) -> p (c g) t q r", g=2, t=PACK, q=BLOCKS),
+                out=ew_sorted[g][:].bitcast(I32).rearrange("p c (t q r) -> p c t q r", t=PACK, q=BLOCKS),
+                in_=ew_raw[g][:].rearrange("p c (q t r) -> p c t q r", t=PACK, q=BLOCKS),
             )
 
         w_t, w_codes, w_scales = {}, {}, {}
 
-        def interleave_w(g):
-            w_t[g] = staged("w_t", [P, K_PASS * PACK], BF16, 2)
-            nc.vector.tensor_copy(
-                out=w_t[g][:].rearrange("p (t q r j) -> p t q r j", t=PACK, r=RUN, j=PACK),
-                in_=w_raw[g][:].rearrange("p j (q t r) -> p t q r j", t=PACK, r=RUN),
-            )
+        def interleave_w(g, part, parts):
+            if part == 0:
+                w_t[g] = staged("w_t", [P, K_PASS * PACK], BF16, 2)
+            dst = w_t[g][:].rearrange("p (t a q h i j) -> p a h t q j i", t=PACK, a=parts, h=2, i=4, j=PACK)
+            src = w_raw[g, part][:].rearrange("p j (q t h i) -> p h t q j i", t=PACK, h=2, i=4)
+            for h in range(2):
+                nc.vector.tensor_copy(out=dst[:, part, h], in_=src[:, h])
 
         def quantize_w(g):
             w_codes[g] = staged("w_codes", [P, K_PASS], U32, 2)
@@ -194,12 +219,12 @@ def tile_log_saturated_latent_scoring_s11_kernel(tc, xq, e_words, e_scales, idf,
 
         d_t, d_codes, d_scales = {}, {}, {}
 
-        def make_d(g, doc_tile, on_vector=False):
+        def make_d(g, doc_tile, on_vector=False, own_bank=None):
             h, n = divmod(doc_tile, DOC_TILES)
-            if n == 0:
+            if (g, h) not in d_t:
                 d_t[g, h] = staged("d_t", [P, HALF, PACK], BF16, 3)
             docs = slice(n * P, (n + 1) * P)
-            bank = new_bank(on_vector)
+            bank = new_bank(on_vector if own_bank is None else own_bank, [P, PACK, P])
             for t in range(PACK):
                 terms = slice(t * P, (t + 1) * P)
                 nc.tensor.matmul_mx(
@@ -215,175 +240,246 @@ def tile_log_saturated_latent_scoring_s11_kernel(tc, xq, e_words, e_scales, idf,
             d_scales[g, h] = kept("d_scales%d_%d" % (g, h), [P, HALF], U8)
             quantize(d_codes[g, h][:], d_scales[g, h][:], d_t[g, h][:].rearrange("m n t -> m (n t)"))
 
+        z_pos = [kept("z_pos%d" % g, [P, PACK, Q], F32) for g in range(GROUPS)]
+        z_bank, z_log, u_t, u_codes, u_scales = {}, {}, {}, {}, {}
+
+        def z_pass(g, t, c, on_vector):
+            part = min(g // 2, 1)
+            if c == 0:
+                z_bank[g, t] = new_bank(on_vector, [P, Q])
+            nc.tensor.matmul_mx(
+                out=z_bank[g, t][:],
+                lhsT=ew_sorted[g][:, c, 2 * P * t : 2 * P * (t + 1)].bitcast(FP4X4),
+                lhsT_scale=es_sorted[part][:, c, g - es_spans[part][0], P * t : P * (t + 1)],
+                rhs=xq_codes[:, c, :].bitcast(FP8X4), rhs_scale=xq_scales[:, c, :],
+                start=(c == 0), stop=(c == H_PASSES - 1),
+            )
+
+        def relu_z(g, t, on_vector):
+            if on_vector:
+                nc.vector.tensor_scalar(out=z_pos[g][:, t, :], in0=z_bank[g, t][:], scalar1=0.0, scalar2=None, op0=ALU.max)
+            else:
+                nc.scalar.activation(out=z_pos[g][:, t, :], in_=z_bank[g, t][:], func=ACT.Relu)
+
+        def make_z(g, t, on_vector):
+            for c in range(H_PASSES):
+                z_pass(g, t, c, on_vector)
+            relu_z(g, t, on_vector)
+
         units = [((g, 0), (g, 1)) for g in range(GROUPS)]
         units = units + [((g, i), (g + 1, i)) for i in (2, 3) for g in range(0, GROUPS, 2)]
-        z_pos, z_log, u_t, u_codes, u_scales = {}, {}, {}, {}, {}
-
-        def make_z(u, b, on_vector):
-            g, i = units[u][b]
-            if b == 0:
-                z_pos[u] = staged("z_pos", [P, 2, P, PACK], F32, 2)
-            bank = new_bank(on_vector)
-            for t in range(PACK):
-                for c in range(H_PASSES):
-                    qs = slice(c * P, (c + 1) * P)
-                    nc.tensor.matmul_mx(
-                        out=bank[:, t, :],
-                        lhsT=ew_sorted[g // 2][:, 2 * c + g % 2, 2 * P * t : 2 * P * (t + 1)].bitcast(FP4X4),
-                        lhsT_scale=es_sorted[:, GROUPS * c + g, P * t : P * (t + 1)],
-                        rhs=xq_codes[i][:, qs].bitcast(FP8X4), rhs_scale=xq_scales[i][:, qs],
-                        start=(c == 0), stop=(c == H_PASSES - 1),
-                    )
-            z = bank[:].rearrange("m t n -> m n t")
-            if on_vector:
-                nc.vector.tensor_scalar(out=z_pos[u][:, b, :, :], in0=z, scalar1=0.0, scalar2=None, op0=ALU.max)
-            else:
-                nc.scalar.activation(out=z_pos[u][:, b, :, :], in_=z, func=ACT.Relu)
 
         def log_z(u, b0, b1):
             if b0 == 0:
-                z_log[u] = staged("z_log", [P, 2, P, PACK], F32, 2)
-            nc.scalar.activation(out=z_log[u][:, b0:b1, :, :], in_=z_pos[u][:, b0:b1, :, :], func=ACT.Ln, bias=1.0)
+                z_log[u] = staged("z_log", [P, 2 * P, PACK], F32, 4)
+            g, i = units[u][b0]
+            nc.scalar.activation(
+                out=z_log[u][:, b0 * P : b1 * P, :].rearrange("m (c i) t -> m c t i", i=4),
+                in_=z_pos[g][:, :, i * P : (i + b1 - b0) * P].rearrange("m t (c i) -> m c t i", i=4),
+                func=ACT.Ln, bias=1.0,
+            )
 
         def weigh(u, b0, b1):
             if b0 == 0:
-                u_t[u] = staged("u_t", [P, 2, P, PACK], BF16, 2)
+                u_t[u] = staged("u_t", [P, 2, P, PACK], BF16, 3)
             g0, g1 = units[u][b0][0], units[u][b1 - 1][0]
             factors = idf_cols[:, g0 : g1 + 1, :].unsqueeze(2).to_broadcast([P, b1 - b0, P, PACK])
-            nc.vector.tensor_tensor(out=u_t[u][:, b0:b1, :, :], in0=z_log[u][:, b0:b1, :, :], in1=factors, op=ALU.mult)
+            logs = z_log[u][:, b0 * P : b1 * P, :].rearrange("m (b n) t -> m b n t", n=P)
+            nc.vector.tensor_tensor(out=u_t[u][:, b0:b1, :, :], in0=logs, in1=factors, op=ALU.mult)
 
         def quantize_u(u, b0, b1):
             if b0 == 0:
-                u_codes[u] = staged("u_codes", [P, 2 * P], U32, 4)
-                u_scales[u] = staged("u_scales", [P, 2 * P], U8, 4)
+                u_codes[u] = staged("u_codes", [P, 2 * P], U32, 6)
+                u_scales[u] = staged("u_scales", [P, 2 * P], U8, 6)
             cols = slice(b0 * P, b1 * P)
             quantize(u_codes[u][:, cols], u_scales[u][:, cols], u_t[u][:, b0:b1, :, :].rearrange("m b n t -> m (b n t)"))
 
         acc = {}
+        acc_bank = {(0, 0): 4, (0, 1): 5, (1, 0): 6, (1, 1): 7, (2, 0): 0, (2, 1): 1, (3, 0): 2, (3, 1): 3}
 
-        def score(u, b):
+        def score(u, b, h):
             g, i = units[u][b]
             cols = slice(b * P, (b + 1) * P)
+            if g == 0:
+                acc[i, h] = take_bank(acc_bank[i, h], [P, HALF])
+            nc.tensor.matmul_mx(
+                out=acc[i, h][:],
+                lhsT=u_codes[u][:, cols].bitcast(FP8X4), lhsT_scale=u_scales[u][:, cols],
+                rhs=d_codes[g, h][:].bitcast(FP8X4), rhs_scale=d_scales[g, h][:],
+                start=(g == 0), stop=(g == GROUPS - 1),
+            )
+
+        def score_tile(u, b):
             for h in range(HALVES):
-                if g == 0:
-                    acc[i, h] = sums.tile([P, HALF], F32, name="acc", tag="acc")
-                nc.tensor.matmul_mx(
-                    out=acc[i, h][:],
-                    lhsT=u_codes[u][:, cols].bitcast(FP8X4), lhsT_scale=u_scales[u][:, cols],
-                    rhs=d_codes[g, h][:].bitcast(FP8X4), rhs_scale=d_scales[g, h][:],
-                    start=(g == 0), stop=(g == GROUPS - 1),
-                )
+                score(u, b, h)
 
         def store(i, h, on_vector):
-            result = staged("result", [P, HALF], F32, 4)
+            result = staged("result", [P, HALF], F32, 6)
             copy_out(on_vector, result[:], acc[i, h][:])
             nc.sync.dma_start(out=out[i * P : (i + 1) * P, h * HALF : (h + 1) * HALF], in_=result[:])
 
+        warm_up(18)
+        sort_idf()
         turn_xd(0, 0, False)
-        turn_idf()
-        turn_xd(0, 1, False)
-        interleave_w(0)
+        warm_up(10)
+        interleave_w(0, 0, 2)
+        load_w(3, 0, 1)
+        load_e_words(2)
+        load_e_words(3)
+        interleave_w(0, 1, 2)
         quantize_xd(0, 0, 256)
         quantize_w(0)
-        turn_xd(1, 0, False)
+        turn_xd(0, 1, False)
+        turn_xd(1, 0, True)
+        warm_up(3)
+        quantize_xd(0, 256, 512)
         make_d(0, 0)
         make_d(0, 1)
-        quantize_xd(0, 256, 512)
-        interleave_w(1)
-        turn_xd(1, 1, True)
+        turn_xd(1, 1, False)
+        interleave_w(1, 0, 1)
         make_d(0, 2)
         make_d(0, 3)
+        quantize_xd(1, 0, 256)
         quantize_w(1)
-        quantize_xd(1, 0, 512)
-        turn_xq(0, True)
+        quantize_xd(1, 256, 512)
+        turn_xq(0, 0, False)
         make_d(0, 4)
         make_d(0, 5)
         quantize_d(0, 0)
-        turn_xq(1, True)
-        quantize_xq(0)
+        turn_xq(1, 0, False)
+        interleave_w(2, 0, 1)
         make_d(0, 6)
-        make_d(0, 7)
-        sort_e_scales()
-        quantize_xq(1)
+        make_d(0, 7, True)
+        turn_xq(0, 1, False)
+        make_d(1, 0)
+        make_d(1, 1)
+        sort_e_scales(0)
         sort_e_words(0)
+        turn_xq(1, 1, True)
+        turn_idf()
+        quantize_xq(0)
+        make_d(1, 2)
+        make_d(1, 3)
+        quantize_xq(1)
+        quantize_d(0, 1)
+        make_d(1, 4)
+        quantize_w(2)
+        make_d(1, 5)
+        make_d(1, 6)
+        quantize_d(1, 0)
+        banks[True] = (3,)
+        banks[False] = (0, 1, 2)
 
-        for g in range(1, GROUPS):
-            u = g - 1
+        for g in range(2, GROUPS):
+            u = g - 2
             more = g + 1 < GROUPS
+            if g + 2 < GROUPS:
+                load_w(g + 2, 0, 1)
+            make_z(u, 0, False)
+            make_d(g - 1, 7, True)
+            make_z(u, 1, False)
             make_d(g, 0)
-            if more:
-                interleave_w(g + 1)
-            else:
-                turn_xq(2, True)
-            make_d(g, 1)
-            if u >= 1:
-                log_z(u - 1, 0, 2)
-            quantize_d(g - 1, 1)
-            make_d(g, 2)
-            make_d(g, 3)
-            make_z(u, 0, True)
-            make_d(g, 4)
-            if u >= 2:
-                score(u - 2, 0)
-            if more:
-                quantize_w(g + 1)
-            else:
-                quantize_xq(2)
-            make_d(g, 5)
             if u >= 1:
                 weigh(u - 1, 0, 2)
-            make_z(u, 1, True)
-            make_d(g, 6)
-            quantize_d(g, 0)
-            make_d(g, 7)
+            else:
+                sort_e_scales(1)
+            quantize_d(g - 1, 1)
+            if u >= 2:
+                score(u - 2, 0, 1)
+                score(u - 2, 1, 0)
+            make_d(g, 3, True)
+            make_z(u, 2, False)
+            make_d(g, 1)
             if u >= 1:
                 quantize_u(u - 1, 0, 2)
+            sort_e_words(u + 1)
+            if u + 4 < GROUPS:
+                load_e_words(u + 4)
             if u >= 2:
-                score(u - 2, 1)
-            if g in (2, 4):
-                sort_e_words(g // 2)
-
-        banks[True] = (3, 2)
-        banks[False] = (0, 1)
-        last = len(units) - 1
-        first = GROUPS - 1
-        for u in range(first, last + 1):
-            log_z(u - 1, 0, 2)
-            make_z(u, 0, True)
-            if u == first:
-                quantize_d(GROUPS - 1, 1)
+                score(u - 2, 1, 1)
+            make_z(u, 3, False)
+            if more:
+                interleave_w(g + 1, 0, 1)
             else:
-                quantize_u(u - 2, 0, 2)
-            make_z(u, 1, False)
-            if u == first:
-                turn_xq(3, False)
-            weigh(u - 1, 0, 2)
-            if u == first + 1:
-                quantize_xq(3)
-            if u > first:
-                score(u - 3, 0)
-                score(u - 3, 1)
-            if u == 8:
-                store(0, 0, False)
-                store(0, 1, True)
-            if u == 9:
-                store(1, 0, False)
-            if u == 10:
-                store(1, 1, False)
-        log_z(last, 0, 1)
-        log_z(last, 1, 2)
-        weigh(last, 0, 1)
-        quantize_u(last - 1, 0, 2)
-        score(last - 2, 0)
-        score(last - 2, 1)
+                sort_e_words(u + 2)
+            make_d(g, 2)
+            make_d(g, 6, True)
+            if not more:
+                log_z(GROUPS, 0, 1)
+            make_d(g, 4, not more, False)
+            if u >= 1:
+                score(u - 1, 0, 0)
+            if more:
+                quantize_w(g + 1)
+            if not more:
+                log_z(GROUPS, 1, 2)
+                quantize_d(g, 0)
+            make_d(g, 5, not more or u == 0, False)
+            if more:
+                quantize_d(g, 0)
+            log_z(u, 0, 2)
+
+        make_z(4, 0, False)
+        make_d(5, 7, True)
+        make_z(4, 1, False)
+        weigh(3, 0, 2)
+        score(2, 0, 1)
+        make_z(4, 2, False)
+        quantize_d(5, 1)
+        score_tile(2, 1)
+        make_z(4, 3, False)
+        quantize_u(3, 0, 2)
+        make_z(5, 0, True)
+        make_z(5, 1, False)
+        log_z(4, 0, 2)
+        weigh(6, 0, 2)
+        make_z(5, 2, True)
+        make_z(5, 3, False)
+        score_tile(3, 0)
+        score_tile(3, 1)
+        log_z(7, 0, 1)
+        weigh(4, 0, 2)
+        quantize_u(6, 0, 2)
+        log_z(7, 1, 2)
+        log_z(5, 0, 2)
+        quantize_u(4, 0, 2)
+        score_tile(6, 0)
+        score_tile(4, 0)
+        score_tile(4, 1)
+        score_tile(6, 1)
+        weigh(7, 0, 2)
+        log_z(8, 0, 1)
+        log_z(8, 1, 2)
+        weigh(5, 0, 2)
+        quantize_u(7, 0, 2)
+        score_tile(7, 0)
+        score_tile(7, 1)
+        log_z(9, 0, 1)
+        log_z(9, 1, 2)
+        quantize_u(5, 0, 2)
+        weigh(8, 0, 2)
+        score_tile(5, 0)
+        score_tile(5, 1)
+        log_z(10, 0, 1)
+        log_z(10, 1, 2)
+        store(0, 0, False)
+        weigh(9, 0, 1)
+        quantize_u(8, 0, 2)
+        score_tile(8, 0)
+        score_tile(8, 1)
+        log_z(11, 0, 1)
+        store(0, 1, False)
+        log_z(11, 1, 2)
+        halves = [(u, b) for u in (9, 10, 11) for b in range(2)]
+        for n in range(1, len(halves)):
+            weigh(halves[n][0], halves[n][1], halves[n][1] + 1)
+            quantize_u(halves[n - 1][0], halves[n - 1][1], halves[n - 1][1] + 1)
+            score_tile(halves[n - 1][0], halves[n - 1][1])
+        store(1, 0, False)
+        store(1, 1, False)
         store(2, 0, False)
-        weigh(last, 1, 2)
-        score(last - 1, 0)
-        score(last - 1, 1)
-        quantize_u(last, 0, 1)
-        quantize_u(last, 1, 2)
-        store(2, 1, False)
-        score(last, 0)
-        score(last, 1)
+        store(2, 1, True)
+        quantize_u(11, 1, 2)
+        score_tile(11, 1)
         store(3, 0, False)
         store(3, 1, True)

@@ -63,15 +63,15 @@ def tile_log_saturated_latent_scoring_s11_kernel(tc, xq, e_words, e_scales, idf,
         def quantize(codes, scales, values):
             nc.vector.quantize_mx(out=codes.bitcast(FP8X4), scales=scales, in_=values)
 
+        zeros = kept("zeros", [P, P * PACK], BF16)
+        nc.gpsimd.memset(zeros[:].bitcast(I32), 0)
         ident = kept("ident", [P, P], F32)
         make_identity(nc, ident[:])
-        idf_rows = kept("idf_rows", [P, K_PASS], F32)
-        nc.gpsimd.memset(idf_rows[:], 0.0)
-        zeros = kept("zeros", [P, P * PACK], BF16)
-        nc.vector.memset(zeros[:], 0.0)
         zero_codes = kept("zero_codes", [P, P], U32)
         zero_scales = kept("zero_scales", [P, P], U8)
         quantize(zero_codes[:], zero_scales[:], zeros[:])
+        idf_rows = kept("idf_rows", [P, K_PASS], F32)
+        nc.vector.memset(idf_rows[:], 0.0)
         es_spans = ((0, 2), (2, GROUPS))
         es_raw = [kept("es_raw%d" % g0, [P, H_PASSES, (g1 - g0) * K_PASS], U8) for g0, g1 in es_spans]
         for plane in es_raw:
@@ -85,7 +85,7 @@ def tile_log_saturated_latent_scoring_s11_kernel(tc, xq, e_words, e_scales, idf,
 
         def load_w(g, part, parts):
             width = K_PASS // parts
-            w_raw[g, part] = staged("w_raw", [P, PACK, width], BF16, 4)
+            w_raw[g, part] = staged("w_raw", [P, PACK, width], BF16, 3)
             cols = slice(g * K_PASS + part * width, g * K_PASS + (part + 1) * width)
             nc.sync.dma_start(out=w_raw[g, part][:], in_=w[:, cols].rearrange("(p j) v -> p j v", j=PACK))
 
@@ -93,11 +93,11 @@ def tile_log_saturated_latent_scoring_s11_kernel(tc, xq, e_words, e_scales, idf,
             xq_raw[i] = kept("xq_raw%d" % i, [P, H], BF16)
             nc.sync.dma_start(out=xq_raw[i][:], in_=xq[i * P : (i + 1) * P, :])
 
-        def load_e_words(g):
-            ew_raw[g] = staged("ew_raw", [P, H_PASSES, 256], I32, 4)
+        def load_e_words(pair):
+            ew_raw[pair] = kept("ew_raw%d" % pair, [P, H_PASSES, K_PASS], I32)
             nc.sync.dma_start(
-                out=ew_raw[g][:],
-                in_=e_words.bitcast(I32)[:, :, g * 256 : (g + 1) * 256].rearrange("c p n -> p c n"),
+                out=ew_raw[pair][:],
+                in_=e_words.bitcast(I32)[:, :, pair * K_PASS : (pair + 1) * K_PASS].rearrange("c p n -> p c n"),
             )
 
         def load_e_scales(part):
@@ -111,7 +111,7 @@ def tile_log_saturated_latent_scoring_s11_kernel(tc, xq, e_words, e_scales, idf,
         idf_raw = kept("idf_raw", [GROUPS, K_PASS], BF16)
         nc.scalar.dma_start(out=idf_raw[:], in_=idf.rearrange("(g v) -> g v", g=GROUPS))
         warm = kept("warm", [P, 1], F32)
-        nc.scalar.activation(out=warm[:], in_=ident[:, 0:1], func=ACT.Ln, bias=1.0)
+        nc.scalar.activation(out=warm[:], in_=zeros[:, 0:1], func=ACT.Ln, bias=1.0)
 
         load_xd(0)
         load_w(0, 0, 2)
@@ -124,11 +124,6 @@ def tile_log_saturated_latent_scoring_s11_kernel(tc, xq, e_words, e_scales, idf,
         load_xq(1)
         load_xq(2)
         load_xq(3)
-        load_w(2, 0, 1)
-        load_e_scales(0)
-        load_e_words(0)
-        load_e_words(1)
-        load_e_scales(1)
 
         def warm_up(passes):
             bank = take_bank(7, [P, PACK, P])
@@ -187,7 +182,7 @@ def tile_log_saturated_latent_scoring_s11_kernel(tc, xq, e_words, e_scales, idf,
             nc.scalar.copy(out=idf_cols[:], in_=bank[:, :, 0:GROUPS].rearrange("m t g -> m g t"))
 
         es_sorted = [kept("es_sorted%d" % g0, [P, H_PASSES, g1 - g0, K_PASS], U8) for g0, g1 in es_spans]
-        ew_sorted = {}
+        ew_sorted = [kept("ew_sorted%d" % pair, [P, H_PASSES * 2, 2 * K_PASS], U8) for pair in range(GROUPS // 2)]
 
         def sort_e_scales(part):
             nc.vector.tensor_copy(
@@ -195,11 +190,10 @@ def tile_log_saturated_latent_scoring_s11_kernel(tc, xq, e_words, e_scales, idf,
                 in_=es_raw[part][:].bitcast(I32).rearrange("p c (g q t r) -> p (c g) t q r", t=PACK, q=BLOCKS, r=2),
             )
 
-        def sort_e_words(g):
-            ew_sorted[g] = staged("ew_sorted", [P, H_PASSES, 2 * K_PASS], U8, 3)
+        def sort_e_words(pair):
             nc.vector.tensor_copy(
-                out=ew_sorted[g][:].bitcast(I32).rearrange("p c (t q r) -> p c t q r", t=PACK, q=BLOCKS),
-                in_=ew_raw[g][:].rearrange("p c (q t r) -> p c t q r", t=PACK, q=BLOCKS),
+                out=ew_sorted[pair][:].bitcast(I32).rearrange("p s (t q r) -> p s t q r", t=PACK, q=BLOCKS),
+                in_=ew_raw[pair][:].rearrange("p c (g q t r) -> p (c g) t q r", g=2, t=PACK, q=BLOCKS),
             )
 
         w_t, w_codes, w_scales = {}, {}, {}
@@ -221,8 +215,8 @@ def tile_log_saturated_latent_scoring_s11_kernel(tc, xq, e_words, e_scales, idf,
 
         def make_d(g, doc_tile, on_vector=False, own_bank=None):
             h, n = divmod(doc_tile, DOC_TILES)
-            if (g, h) not in d_t:
-                d_t[g, h] = staged("d_t", [P, HALF, PACK], BF16, 3)
+            if g not in d_t:
+                d_t[g] = staged("d_t", [P, D, PACK], BF16, 2)
             docs = slice(n * P, (n + 1) * P)
             bank = new_bank(on_vector if own_bank is None else own_bank, [P, PACK, P])
             for t in range(PACK):
@@ -233,38 +227,37 @@ def tile_log_saturated_latent_scoring_s11_kernel(tc, xq, e_words, e_scales, idf,
                     rhs=xd_codes[h][:, docs].bitcast(FP8X4), rhs_scale=xd_scales[h][:, docs],
                     start=True, stop=True,
                 )
-            copy_out(on_vector, d_t[g, h][:, docs, :], bank[:].rearrange("m t n -> m n t"))
+            copy_out(on_vector, d_t[g][:, doc_tile * P : (doc_tile + 1) * P, :], bank[:].rearrange("m t n -> m n t"))
 
-        def quantize_d(g, h):
-            d_codes[g, h] = kept("d_codes%d_%d" % (g, h), [P, HALF], U32)
-            d_scales[g, h] = kept("d_scales%d_%d" % (g, h), [P, HALF], U8)
-            quantize(d_codes[g, h][:], d_scales[g, h][:], d_t[g, h][:].rearrange("m n t -> m (n t)"))
+        def quantize_d(g):
+            d_codes[g] = kept("d_codes%d" % g, [P, D], U32)
+            d_scales[g] = kept("d_scales%d" % g, [P, D], U8)
+            quantize(d_codes[g][:], d_scales[g][:], d_t[g][:].rearrange("m n t -> m (n t)"))
 
-        z_pos = [kept("z_pos%d" % g, [P, PACK, Q], F32) for g in range(GROUPS)]
-        z_bank, z_log, u_t, u_codes, u_scales = {}, {}, {}, {}, {}
+        z_late = {i: kept("z_late%d" % i, [P, GROUPS, P, PACK], F32) for i in (2, 3)}
+        z_early, z_log, u_t, u_codes, u_scales = {}, {}, {}, {}, {}
 
-        def z_pass(g, t, c, on_vector):
+        def make_z(g, i, on_vector):
             part = min(g // 2, 1)
-            if c == 0:
-                z_bank[g, t] = new_bank(on_vector, [P, Q])
-            nc.tensor.matmul_mx(
-                out=z_bank[g, t][:],
-                lhsT=ew_sorted[g][:, c, 2 * P * t : 2 * P * (t + 1)].bitcast(FP4X4),
-                lhsT_scale=es_sorted[part][:, c, g - es_spans[part][0], P * t : P * (t + 1)],
-                rhs=xq_codes[:, c, :].bitcast(FP8X4), rhs_scale=xq_scales[:, c, :],
-                start=(c == 0), stop=(c == H_PASSES - 1),
-            )
-
-        def relu_z(g, t, on_vector):
+            if i == 0:
+                z_early[g] = staged("z_early", [P, 2, P, PACK], F32, 2)
+            bank = new_bank(on_vector, [P, PACK, P])
+            qs = slice(i * P, (i + 1) * P)
+            for t in range(PACK):
+                for c in range(H_PASSES):
+                    nc.tensor.matmul_mx(
+                        out=bank[:, t, :],
+                        lhsT=ew_sorted[g // 2][:, 2 * c + g % 2, 2 * P * t : 2 * P * (t + 1)].bitcast(FP4X4),
+                        lhsT_scale=es_sorted[part][:, c, g - es_spans[part][0], P * t : P * (t + 1)],
+                        rhs=xq_codes[:, c, qs].bitcast(FP8X4), rhs_scale=xq_scales[:, c, qs],
+                        start=(c == 0), stop=(c == H_PASSES - 1),
+                    )
+            dst = z_early[g][:, i, :, :] if i < 2 else z_late[i][:, g, :, :]
+            z = bank[:].rearrange("m t n -> m n t")
             if on_vector:
-                nc.vector.tensor_scalar(out=z_pos[g][:, t, :], in0=z_bank[g, t][:], scalar1=0.0, scalar2=None, op0=ALU.max)
+                nc.vector.tensor_scalar(out=dst, in0=z, scalar1=0.0, scalar2=None, op0=ALU.max)
             else:
-                nc.scalar.activation(out=z_pos[g][:, t, :], in_=z_bank[g, t][:], func=ACT.Relu)
-
-        def make_z(g, t, on_vector):
-            for c in range(H_PASSES):
-                z_pass(g, t, c, on_vector)
-            relu_z(g, t, on_vector)
+                nc.scalar.activation(out=dst, in_=z, func=ACT.Relu)
 
         units = [((g, 0), (g, 1)) for g in range(GROUPS)]
         units = units + [((g, i), (g + 1, i)) for i in (2, 3) for g in range(0, GROUPS, 2)]
@@ -272,10 +265,11 @@ def tile_log_saturated_latent_scoring_s11_kernel(tc, xq, e_words, e_scales, idf,
         def log_z(u, b0, b1):
             if b0 == 0:
                 z_log[u] = staged("z_log", [P, 2 * P, PACK], F32, 4)
-            g, i = units[u][b0]
+            g, i = units[u][0]
+            src = z_early[g] if i < 2 else z_late[i][:, g : g + 2, :, :]
             nc.scalar.activation(
-                out=z_log[u][:, b0 * P : b1 * P, :].rearrange("m (c i) t -> m c t i", i=4),
-                in_=z_pos[g][:, :, i * P : (i + b1 - b0) * P].rearrange("m t (c i) -> m c t i", i=4),
+                out=z_log[u][:, b0 * P : b1 * P, :].rearrange("m n t -> m (n t)"),
+                in_=src[:, b0:b1, :, :].rearrange("m b n t -> m (b n t)"),
                 func=ACT.Ln, bias=1.0,
             )
 
@@ -300,12 +294,13 @@ def tile_log_saturated_latent_scoring_s11_kernel(tc, xq, e_words, e_scales, idf,
         def score(u, b, h):
             g, i = units[u][b]
             cols = slice(b * P, (b + 1) * P)
+            docs = slice(h * HALF, (h + 1) * HALF)
             if g == 0:
                 acc[i, h] = take_bank(acc_bank[i, h], [P, HALF])
             nc.tensor.matmul_mx(
                 out=acc[i, h][:],
                 lhsT=u_codes[u][:, cols].bitcast(FP8X4), lhsT_scale=u_scales[u][:, cols],
-                rhs=d_codes[g, h][:].bitcast(FP8X4), rhs_scale=d_scales[g, h][:],
+                rhs=d_codes[g][:, docs].bitcast(FP8X4), rhs_scale=d_scales[g][:, docs],
                 start=(g == 0), stop=(g == GROUPS - 1),
             )
 
@@ -318,15 +313,18 @@ def tile_log_saturated_latent_scoring_s11_kernel(tc, xq, e_words, e_scales, idf,
             copy_out(on_vector, result[:], acc[i, h][:])
             nc.sync.dma_start(out=out[i * P : (i + 1) * P, h * HALF : (h + 1) * HALF], in_=result[:])
 
-        warm_up(18)
+        warm_up(12)
         sort_idf()
         turn_xd(0, 0, False)
-        warm_up(10)
+        warm_up(8)
         interleave_w(0, 0, 2)
-        load_w(3, 0, 1)
-        load_e_words(2)
-        load_e_words(3)
+        load_w(2, 0, 1)
+        load_e_scales(0)
+        load_e_words(0)
+        load_e_scales(1)
         interleave_w(0, 1, 2)
+        load_w(3, 0, 1)
+        load_e_words(1)
         quantize_xd(0, 0, 256)
         quantize_w(0)
         turn_xd(0, 1, False)
@@ -337,17 +335,19 @@ def tile_log_saturated_latent_scoring_s11_kernel(tc, xq, e_words, e_scales, idf,
         make_d(0, 1)
         turn_xd(1, 1, False)
         interleave_w(1, 0, 1)
+        load_w(4, 0, 1)
+        load_e_words(2)
         make_d(0, 2)
         make_d(0, 3)
         quantize_xd(1, 0, 256)
         quantize_w(1)
         quantize_xd(1, 256, 512)
         turn_xq(0, 0, False)
-        make_d(0, 4)
+        make_d(0, 4, True)
         make_d(0, 5)
-        quantize_d(0, 0)
         turn_xq(1, 0, False)
         interleave_w(2, 0, 1)
+        load_w(5, 0, 1)
         make_d(0, 6)
         make_d(0, 7, True)
         turn_xq(0, 1, False)
@@ -361,125 +361,113 @@ def tile_log_saturated_latent_scoring_s11_kernel(tc, xq, e_words, e_scales, idf,
         make_d(1, 2)
         make_d(1, 3)
         quantize_xq(1)
-        quantize_d(0, 1)
+        quantize_d(0)
         make_d(1, 4)
-        quantize_w(2)
         make_d(1, 5)
         make_d(1, 6)
-        quantize_d(1, 0)
         banks[True] = (3,)
         banks[False] = (0, 1, 2)
 
         for g in range(2, GROUPS):
             u = g - 2
             more = g + 1 < GROUPS
-            if g + 2 < GROUPS:
-                load_w(g + 2, 0, 1)
-            make_z(u, 0, False)
             make_d(g - 1, 7, True)
+            quantize_w(g)
+            make_z(u, 0, False)
             make_z(u, 1, False)
-            make_d(g, 0)
+            make_z(u, 2, False)
             if u >= 1:
                 weigh(u - 1, 0, 2)
             else:
                 sort_e_scales(1)
-            quantize_d(g - 1, 1)
-            if u >= 2:
-                score(u - 2, 0, 1)
-                score(u - 2, 1, 0)
-            make_d(g, 3, True)
-            make_z(u, 2, False)
+            if u < 2:
+                make_z(2 * u, 3, True)
+            else:
+                score_tile(u - 2, 0)
+            make_d(g, 0)
+            quantize_d(g - 1)
             make_d(g, 1)
+            if u >= 2:
+                score(u - 2, 1, 0)
             if u >= 1:
                 quantize_u(u - 1, 0, 2)
-            sort_e_words(u + 1)
-            if u + 4 < GROUPS:
-                load_e_words(u + 4)
+            make_d(g, 2)
+            if u < 2:
+                make_z(2 * u + 1, 3, True)
+            else:
+                make_d(g, 6, True)
+            make_d(g, 3)
             if u >= 2:
                 score(u - 2, 1, 1)
-            make_z(u, 3, False)
+            if u % 2 == 0:
+                sort_e_words(u // 2 + 1)
             if more:
                 interleave_w(g + 1, 0, 1)
             else:
-                sort_e_words(u + 2)
-            make_d(g, 2)
-            make_d(g, 6, True)
-            if not more:
-                log_z(GROUPS, 0, 1)
+                log_z(GROUPS, 0, 2)
             make_d(g, 4, not more, False)
-            if u >= 1:
-                score(u - 1, 0, 0)
-            if more:
-                quantize_w(g + 1)
-            if not more:
-                log_z(GROUPS, 1, 2)
-                quantize_d(g, 0)
-            make_d(g, 5, not more or u == 0, False)
-            if more:
-                quantize_d(g, 0)
+            make_d(g, 5, not more, False)
+            if u < 2:
+                make_d(g, 6, u == 1, False)
             log_z(u, 0, 2)
 
-        make_z(4, 0, False)
         make_d(5, 7, True)
+        make_z(4, 0, False)
         make_z(4, 1, False)
-        weigh(3, 0, 2)
-        score(2, 0, 1)
         make_z(4, 2, False)
-        quantize_d(5, 1)
-        score_tile(2, 1)
-        make_z(4, 3, False)
-        quantize_u(3, 0, 2)
-        make_z(5, 0, True)
-        make_z(5, 1, False)
-        log_z(4, 0, 2)
+        banks[False] = (2, 3)
+        banks[True] = (2, 3)
         weigh(6, 0, 2)
-        make_z(5, 2, True)
-        make_z(5, 3, False)
+        weigh(3, 0, 2)
+        log_z(4, 0, 2)
+        make_z(5, 0, False)
+        score_tile(2, 0)
+        score_tile(2, 1)
+        make_z(5, 1, False)
+        quantize_u(6, 0, 2)
+        quantize_u(3, 0, 2)
+        quantize_d(5)
         score_tile(3, 0)
         score_tile(3, 1)
-        log_z(7, 0, 1)
         weigh(4, 0, 2)
-        quantize_u(6, 0, 2)
-        log_z(7, 1, 2)
+        make_z(5, 2, True)
+        log_z(7, 0, 2)
         log_z(5, 0, 2)
-        quantize_u(4, 0, 2)
+        make_z(4, 3, False)
         score_tile(6, 0)
-        score_tile(4, 0)
-        score_tile(4, 1)
+        make_z(5, 3, False)
         score_tile(6, 1)
         weigh(7, 0, 2)
-        log_z(8, 0, 1)
-        log_z(8, 1, 2)
+        quantize_u(4, 0, 2)
+        score_tile(4, 0)
+        score_tile(4, 1)
+        log_z(8, 0, 2)
         weigh(5, 0, 2)
         quantize_u(7, 0, 2)
-        score_tile(7, 0)
-        score_tile(7, 1)
-        log_z(9, 0, 1)
-        log_z(9, 1, 2)
         quantize_u(5, 0, 2)
-        weigh(8, 0, 2)
         score_tile(5, 0)
         score_tile(5, 1)
-        log_z(10, 0, 1)
-        log_z(10, 1, 2)
-        store(0, 0, False)
+        score_tile(7, 0)
+        score_tile(7, 1)
+        log_z(9, 0, 2)
+        weigh(8, 0, 2)
+        log_z(10, 0, 2)
+        log_z(11, 0, 2)
+        halves = [(u, b) for u in (9, 10, 11) for b in range(2)]
         weigh(9, 0, 1)
         quantize_u(8, 0, 2)
         score_tile(8, 0)
         score_tile(8, 1)
-        log_z(11, 0, 1)
-        store(0, 1, False)
-        log_z(11, 1, 2)
-        halves = [(u, b) for u in (9, 10, 11) for b in range(2)]
         for n in range(1, len(halves)):
             weigh(halves[n][0], halves[n][1], halves[n][1] + 1)
             quantize_u(halves[n - 1][0], halves[n - 1][1], halves[n - 1][1] + 1)
-            score_tile(halves[n - 1][0], halves[n - 1][1])
-        store(1, 0, False)
-        store(1, 1, False)
-        store(2, 0, False)
-        store(2, 1, True)
+            if n + 1 < len(halves):
+                score_tile(halves[n - 1][0], halves[n - 1][1])
+        for i in range(3):
+            for h in range(HALVES):
+                store(i, h, False)
         quantize_u(11, 1, 2)
-        score_tile(11, 1)
-        store(3, 0, False)
-        store(3, 1, True)
+        for h in range(HALVES):
+            score(11, 0, h)
+            score(11, 1, h)
+            store(3, h, h == 0)

@@ -17,16 +17,22 @@ ALU = mybir.AluOpType
 ACT = mybir.ActivationFunctionType
 
 P = 128
-PACK = 4
-K_PASS = P * PACK
+SLOTS = 4
+K_PASS = P * SLOTS
 GROUPS = V // K_PASS
 H_PASSES = H // K_PASS
-Q_TILES = Q // P
-HALF = 512
-HALVES = D // HALF
-DOC_TILES = HALF // P
 RUN = 8
 BLOCKS = P // RUN
+HALF = 512
+HALVES = D // HALF
+PAIR = 2 * P
+PAIR_WORDS = K_PASS // 2
+BANKS = 8
+WARM_BANK = BANKS - 1
+WARM_N = 256
+WARM_FIRST, WARM_SECOND, WARM_THIRD = 7, 6, 4
+D_AHEAD = 2
+SCALAR, VECTOR = False, True
 
 
 def tile_log_saturated_latent_scoring_s11_kernel(tc, xq, e_words, e_scales, idf, xd, w, out):
@@ -43,19 +49,19 @@ def tile_log_saturated_latent_scoring_s11_kernel(tc, xq, e_words, e_scales, idf,
         def staged(tag, shape, dtype, bufs):
             return stage.tile(shape, dtype, name=tag, tag=tag, bufs=bufs, align_bytes=64)
 
-        oldest_first = list(range(8))
-        banks = {True: (3, 4), False: (0, 1, 2, 5, 6)}
+        oldest_first = list(range(BANKS))
+        banks_of = {SCALAR: range(WARM_BANK), VECTOR: range(WARM_BANK)}
 
         def take_bank(b, shape):
             oldest_first.remove(b)
             oldest_first.append(b)
             return psum.tile(shape, F32, name="bank%d" % b, tag="bank%d" % b)
 
-        def new_bank(on_vector, shape):
-            return take_bank([b for b in oldest_first if b in banks[on_vector]][0], shape)
+        def slot_bank(owner):
+            return take_bank([b for b in oldest_first if b in banks_of[owner]][0], [P, SLOTS, P])
 
-        def copy_out(on_vector, dst, src):
-            if on_vector:
+        def copy_out(reader, dst, src):
+            if reader == VECTOR:
                 nc.vector.tensor_copy(out=dst, in_=src)
             else:
                 nc.scalar.copy(out=dst, in_=src)
@@ -63,148 +69,157 @@ def tile_log_saturated_latent_scoring_s11_kernel(tc, xq, e_words, e_scales, idf,
         def quantize(codes, scales, values):
             nc.vector.quantize_mx(out=codes.bitcast(FP8X4), scales=scales, in_=values)
 
-        zeros = kept("zeros", [P, P * PACK], BF16)
+        zeros = kept("zeros", [P, WARM_N * SLOTS], BF16)
         nc.gpsimd.memset(zeros[:].bitcast(I32), 0)
+        zero_codes = kept("zero_codes", [P, WARM_N], U32)
+        zero_scales = kept("zero_scales", [P, WARM_N], U8)
+        quantize(zero_codes[:], zero_scales[:], zeros[:])
         ident = kept("ident", [P, P], F32)
         make_identity(nc, ident[:])
-        zero_codes = kept("zero_codes", [P, P], U32)
-        zero_scales = kept("zero_scales", [P, P], U8)
-        quantize(zero_codes[:], zero_scales[:], zeros[:])
         idf_rows = kept("idf_rows", [P, K_PASS], F32)
         nc.vector.memset(idf_rows[:], 0.0)
         es_spans = ((0, 2), (2, GROUPS))
         es_raw = [kept("es_raw%d" % g0, [P, H_PASSES, (g1 - g0) * K_PASS], U8) for g0, g1 in es_spans]
-        for plane in es_raw:
-            nc.vector.memset(plane[:].bitcast(I32), 0)
+        for raw in es_raw:
+            nc.vector.memset(raw[:].bitcast(I32), 0)
 
         xd_raw, w_raw, xq_raw, ew_raw = {}, {}, {}, {}
 
-        def load_xd(part):
-            xd_raw[part] = kept("xd_raw%d" % part, [P, 2 * L], BF16)
-            nc.sync.dma_start(out=xd_raw[part][:], in_=xd[part * 256 : (part + 1) * 256, :].rearrange("(p a) k -> p (a k)", a=2))
+        def load_xd(pair):
+            xd_raw[pair] = kept("xd_raw%d" % pair, [P, 2 * L], BF16)
+            rows = xd[pair * PAIR : (pair + 1) * PAIR, :]
+            nc.sync.dma_start(out=xd_raw[pair][:], in_=rows.rearrange("(p a) k -> p (a k)", a=2))
 
-        def load_w(g, part, parts):
-            width = K_PASS // parts
-            w_raw[g, part] = staged("w_raw", [P, PACK, width], BF16, 3)
-            cols = slice(g * K_PASS + part * width, g * K_PASS + (part + 1) * width)
-            nc.sync.dma_start(out=w_raw[g, part][:], in_=w[:, cols].rearrange("(p j) v -> p j v", j=PACK))
+        def load_w(g):
+            w_raw[g] = staged("w_raw", [P, SLOTS, K_PASS], BF16, 3)
+            cols = w[:, g * K_PASS : (g + 1) * K_PASS]
+            nc.sync.dma_start(out=w_raw[g][:], in_=cols.rearrange("(p j) v -> p j v", j=SLOTS))
 
         def load_xq(i):
             xq_raw[i] = kept("xq_raw%d" % i, [P, H], BF16)
             nc.sync.dma_start(out=xq_raw[i][:], in_=xq[i * P : (i + 1) * P, :])
 
-        def load_e_words(pair):
-            ew_raw[pair] = kept("ew_raw%d" % pair, [P, H_PASSES, K_PASS], I32)
+        def load_e_words(n):
+            ew_raw[n] = kept("ew_raw%d" % n, [P, H_PASSES, K_PASS], I32)
             nc.sync.dma_start(
-                out=ew_raw[pair][:],
-                in_=e_words.bitcast(I32)[:, :, pair * K_PASS : (pair + 1) * K_PASS].rearrange("c p n -> p c n"),
+                out=ew_raw[n][:],
+                in_=e_words.bitcast(I32)[:, :, n * K_PASS : (n + 1) * K_PASS].rearrange("c p v -> p c v"),
             )
 
         def load_e_scales(part):
             g0, g1 = es_spans[part]
-            for quad in range(4):
+            for j in range(4):
+                rows = e_scales[:, 4 * j : 4 * j + 4, g0 * K_PASS : g1 * K_PASS]
                 nc.sync.dma_start(
-                    out=es_raw[part][32 * quad : 32 * quad + 4, :, :].bitcast(I32),
-                    in_=e_scales[:, 4 * quad : 4 * quad + 4, g0 * K_PASS : g1 * K_PASS].bitcast(I32).rearrange("c r n -> r c n"),
+                    out=es_raw[part][32 * j : 32 * j + 4, :, :].bitcast(I32),
+                    in_=rows.bitcast(I32).rearrange("c r v -> r c v"),
                 )
 
         idf_raw = kept("idf_raw", [GROUPS, K_PASS], BF16)
         nc.scalar.dma_start(out=idf_raw[:], in_=idf.rearrange("(g v) -> g v", g=GROUPS))
-        warm = kept("warm", [P, 1], F32)
-        nc.scalar.activation(out=warm[:], in_=zeros[:, 0:1], func=ACT.Ln, bias=1.0)
+        ln_table = kept("ln_table", [P, 1], F32)
+        nc.scalar.activation(out=ln_table[:], in_=zeros[:, 0:1], func=ACT.Ln, bias=1.0)
 
         load_xd(0)
-        load_w(0, 0, 2)
-        load_w(0, 1, 2)
-        load_xd(1)
-        load_xd(2)
-        load_xd(3)
-        load_w(1, 0, 1)
-        load_xq(0)
-        load_xq(1)
-        load_xq(2)
-        load_xq(3)
+        load_w(0)
+        for pair in range(1, D // PAIR):
+            load_xd(pair)
+        load_w(1)
+        for i in range(Q // P):
+            load_xq(i)
+        load_w(2)
 
         def warm_up(passes):
-            bank = take_bank(7, [P, PACK, P])
+            bank = take_bank(WARM_BANK, [P, WARM_N])
             for n in range(passes):
                 nc.tensor.matmul_mx(
-                    out=bank[:, n % PACK, :],
-                    lhsT=zero_codes[:].bitcast(FP8X4), lhsT_scale=zero_scales[:],
+                    out=bank[:],
+                    lhsT=zero_codes[:, 0:P].bitcast(FP8X4), lhsT_scale=zero_scales[:, 0:P],
                     rhs=zero_codes[:].bitcast(FP8X4), rhs_scale=zero_scales[:],
                     start=True, stop=True,
                 )
 
-        xd_t = [kept("xd_t%d" % h, [P, HALF, PACK], BF16) for h in range(HALVES)]
+        xd_t = [kept("xd_t%d" % h, [P, HALF, SLOTS], BF16) for h in range(HALVES)]
         xd_codes = [kept("xd_codes%d" % h, [P, HALF], U32) for h in range(HALVES)]
         xd_scales = [kept("xd_scales%d" % h, [P, HALF], U8) for h in range(HALVES)]
 
-        def turn_xd(h, n, on_vector):
-            words = xd_raw[2 * h + n][:].bitcast(F32)
-            bank = new_bank(on_vector, [P, PACK, P])
+        def pair_docs(pair):
+            h, n = divmod(pair, HALF // PAIR)
+            return h, slice(n * PAIR, (n + 1) * PAIR)
+
+        def turn_xd(pair, reader):
+            h, docs = pair_docs(pair)
+            words = xd_raw[pair][:].bitcast(F32)
+            bank = slot_bank(reader)
             for a in range(2):
-                for u in range(2):
-                    nc.tensor.transpose(bank[:, 2 * a + u, :], words[:, 256 * a + u : 256 * (a + 1) : 2], ident[:])
-            dst = xd_t[h][:, 256 * n : 256 * (n + 1), :].rearrange("k d t -> k (d t)").bitcast(F32)
-            copy_out(on_vector, dst.rearrange("k (p j) -> k p j", j=PACK), bank[:].rearrange("k j p -> k p j"))
+                for odd in range(2):
+                    src = words[:, PAIR_WORDS * a + odd : PAIR_WORDS * (a + 1) : 2]
+                    nc.tensor.transpose(bank[:, 2 * a + odd, :], src, ident[:])
+            dst = xd_t[h][:, docs, :].rearrange("k d t -> k (d t)").bitcast(F32)
+            copy_out(reader, dst.rearrange("k (p j) -> k p j", j=4), bank[:].rearrange("k j p -> k p j"))
 
-        def quantize_xd(h, d0, d1):
-            quantize(xd_codes[h][:, d0:d1], xd_scales[h][:, d0:d1], xd_t[h][:, d0:d1, :].rearrange("k d t -> k (d t)"))
+        def quantize_xd(pair):
+            h, docs = pair_docs(pair)
+            quantize(xd_codes[h][:, docs], xd_scales[h][:, docs], xd_t[h][:, docs, :].rearrange("k d t -> k (d t)"))
 
-        xq_t = [kept("xq_t%d" % c, [P, Q * PACK], BF16) for c in range(H_PASSES)]
-        xq_codes = kept("xq_codes", [P, H_PASSES, Q], U32)
-        xq_scales = kept("xq_scales", [P, H_PASSES, Q], U8)
+        xq_t = [kept("xq_t%d" % pair, [P, H_PASSES, PAIR * SLOTS], BF16) for pair in range(Q // PAIR)]
+        xq_codes = [kept("xq_codes%d" % pair, [P, H_PASSES, PAIR], U32) for pair in range(Q // PAIR)]
+        xq_scales = [kept("xq_scales%d" % pair, [P, H_PASSES, PAIR], U8) for pair in range(Q // PAIR)]
 
-        def turn_xq(c, pair, on_vector):
-            bank = new_bank(on_vector, [P, PACK, P])
+        def turn_xq(pair, c, reader):
+            bank = slot_bank(reader)
             for a in range(2):
                 words = xq_raw[2 * pair + a][:].bitcast(F32)
-                for u in range(2):
-                    nc.tensor.transpose(bank[:, 2 * a + u, :], words[:, 256 * c + u : 256 * (c + 1) : 2], ident[:])
-            dst = xq_t[c][:, 1024 * pair : 1024 * (pair + 1)].bitcast(F32)
-            copy_out(on_vector, dst.rearrange("k (a q u) -> k a q u", a=2, u=2), bank[:].rearrange("k (a u) q -> k a q u", u=2))
+                for odd in range(2):
+                    src = words[:, PAIR_WORDS * c + odd : PAIR_WORDS * (c + 1) : 2]
+                    nc.tensor.transpose(bank[:, 2 * a + odd, :], src, ident[:])
+            dst = xq_t[pair][:, c, :].bitcast(F32)
+            copy_out(reader, dst.rearrange("k (a q o) -> k a q o", a=2, o=2), bank[:].rearrange("k (a o) q -> k a q o", o=2))
 
-        def quantize_xq(c):
-            quantize(xq_codes[:, c, :], xq_scales[:, c, :], xq_t[c][:])
+        def quantize_xq(pair):
+            quantize(
+                xq_codes[pair][:].rearrange("k c q -> k (c q)"),
+                xq_scales[pair][:].rearrange("k c q -> k (c q)"),
+                xq_t[pair][:].rearrange("k c n -> k (c n)"),
+            )
 
-        idf_cols = kept("idf_cols", [P, GROUPS, PACK], F32)
+        idf_cols = kept("idf_cols", [P, GROUPS, SLOTS], F32)
 
         def sort_idf():
             nc.scalar.copy(
-                out=idf_rows[0:GROUPS, :].rearrange("g (t q r) -> g t q r", t=PACK, r=RUN),
-                in_=idf_raw[:].rearrange("g (q t r) -> g t q r", t=PACK, r=RUN),
+                out=idf_rows[0:GROUPS, :].rearrange("g (t b r) -> g t b r", t=SLOTS, r=RUN),
+                in_=idf_raw[:].rearrange("g (b t r) -> g t b r", t=SLOTS, r=RUN),
             )
 
         def turn_idf():
-            bank = new_bank(False, [P, PACK, P])
-            for t in range(PACK):
+            bank = slot_bank(SCALAR)
+            for t in range(SLOTS):
                 nc.tensor.transpose(bank[:, t, :], idf_rows[:, t * P : (t + 1) * P], ident[:])
             nc.scalar.copy(out=idf_cols[:], in_=bank[:, :, 0:GROUPS].rearrange("m t g -> m g t"))
 
         es_sorted = [kept("es_sorted%d" % g0, [P, H_PASSES, g1 - g0, K_PASS], U8) for g0, g1 in es_spans]
-        ew_sorted = [kept("ew_sorted%d" % pair, [P, H_PASSES * 2, 2 * K_PASS], U8) for pair in range(GROUPS // 2)]
+        ew_sorted = [kept("ew_sorted%d" % n, [P, H_PASSES * 2, 2 * K_PASS], U8) for n in range(GROUPS // 2)]
 
         def sort_e_scales(part):
             nc.vector.tensor_copy(
-                out=es_sorted[part][:].bitcast(I32).rearrange("p c g (t q r) -> p (c g) t q r", t=PACK, q=BLOCKS),
-                in_=es_raw[part][:].bitcast(I32).rearrange("p c (g q t r) -> p (c g) t q r", t=PACK, q=BLOCKS, r=2),
+                out=es_sorted[part][:].bitcast(I32).rearrange("p c g (t b r) -> p (c g) t b r", t=SLOTS, b=BLOCKS),
+                in_=es_raw[part][:].bitcast(I32).rearrange("p c (g b t r) -> p (c g) t b r", t=SLOTS, b=BLOCKS, r=2),
             )
 
-        def sort_e_words(pair):
+        def sort_e_words(n):
             nc.vector.tensor_copy(
-                out=ew_sorted[pair][:].bitcast(I32).rearrange("p s (t q r) -> p s t q r", t=PACK, q=BLOCKS),
-                in_=ew_raw[pair][:].rearrange("p c (g q t r) -> p (c g) t q r", g=2, t=PACK, q=BLOCKS),
+                out=ew_sorted[n][:].bitcast(I32).rearrange("p s (t b r) -> p s t b r", t=SLOTS, b=BLOCKS),
+                in_=ew_raw[n][:].rearrange("p c (g b t r) -> p (c g) t b r", g=2, t=SLOTS, b=BLOCKS),
             )
 
         w_t, w_codes, w_scales = {}, {}, {}
 
-        def interleave_w(g, part, parts):
-            if part == 0:
-                w_t[g] = staged("w_t", [P, K_PASS * PACK], BF16, 2)
-            dst = w_t[g][:].rearrange("p (t a q h i j) -> p a h t q j i", t=PACK, a=parts, h=2, i=4, j=PACK)
-            src = w_raw[g, part][:].rearrange("p j (q t h i) -> p h t q j i", t=PACK, h=2, i=4)
-            for h in range(2):
-                nc.vector.tensor_copy(out=dst[:, part, h], in_=src[:, h])
+        def interleave_w(g):
+            w_t[g] = staged("w_t", [P, K_PASS * SLOTS], BF16, 2)
+            nc.vector.tensor_copy(
+                out=w_t[g][:].rearrange("p (t b r j) -> p t b r j", t=SLOTS, r=RUN, j=SLOTS),
+                in_=w_raw[g][:].rearrange("p j (b t r) -> p t b r j", t=SLOTS, r=RUN),
+            )
 
         def quantize_w(g):
             w_codes[g] = staged("w_codes", [P, K_PASS], U32, 2)
@@ -213,13 +228,13 @@ def tile_log_saturated_latent_scoring_s11_kernel(tc, xq, e_words, e_scales, idf,
 
         d_t, d_codes, d_scales = {}, {}, {}
 
-        def make_d(g, doc_tile, on_vector=False, own_bank=None):
-            h, n = divmod(doc_tile, DOC_TILES)
+        def make_d(g, n, reader=SCALAR, owner=None):
+            h, first = divmod(n * P, HALF)
             if g not in d_t:
-                d_t[g] = staged("d_t", [P, D, PACK], BF16, 2)
-            docs = slice(n * P, (n + 1) * P)
-            bank = new_bank(on_vector if own_bank is None else own_bank, [P, PACK, P])
-            for t in range(PACK):
+                d_t[g] = staged("d_t", [P, D, SLOTS], BF16, 2)
+            docs = slice(first, first + P)
+            bank = slot_bank(reader if owner is None else owner)
+            for t in range(SLOTS):
                 terms = slice(t * P, (t + 1) * P)
                 nc.tensor.matmul_mx(
                     out=bank[:, t, :],
@@ -227,247 +242,247 @@ def tile_log_saturated_latent_scoring_s11_kernel(tc, xq, e_words, e_scales, idf,
                     rhs=xd_codes[h][:, docs].bitcast(FP8X4), rhs_scale=xd_scales[h][:, docs],
                     start=True, stop=True,
                 )
-            copy_out(on_vector, d_t[g][:, doc_tile * P : (doc_tile + 1) * P, :], bank[:].rearrange("m t n -> m n t"))
+            copy_out(reader, d_t[g][:, n * P : (n + 1) * P, :], bank[:].rearrange("m t n -> m n t"))
 
         def quantize_d(g):
             d_codes[g] = kept("d_codes%d" % g, [P, D], U32)
             d_scales[g] = kept("d_scales%d" % g, [P, D], U8)
             quantize(d_codes[g][:], d_scales[g][:], d_t[g][:].rearrange("m n t -> m (n t)"))
 
-        z_late = {i: kept("z_late%d" % i, [P, GROUPS, P, PACK], F32) for i in (2, 3)}
+        early = [((g, 0), (g, 1)) for g in range(GROUPS)]
+        late = {i: [((g, i), (g + 1, i)) for g in range(0, GROUPS, 2)] for i in (2, 3)}
+        z_late = {i: kept("z_late%d" % i, [P, GROUPS, P, SLOTS], F32) for i in (2, 3)}
         z_early, z_log, u_t, u_codes, u_scales = {}, {}, {}, {}, {}
 
-        def make_z(g, i, on_vector):
+        def make_z(g, i, reader):
             part = min(g // 2, 1)
             if i == 0:
-                z_early[g] = staged("z_early", [P, 2, P, PACK], F32, 2)
-            bank = new_bank(on_vector, [P, PACK, P])
-            qs = slice(i * P, (i + 1) * P)
-            for t in range(PACK):
+                z_early[g] = staged("z_early", [P, 2, P, SLOTS], F32, 2)
+            bank = slot_bank(reader)
+            queries = slice(i % 2 * P, (i % 2 + 1) * P)
+            for t in range(SLOTS):
                 for c in range(H_PASSES):
                     nc.tensor.matmul_mx(
                         out=bank[:, t, :],
                         lhsT=ew_sorted[g // 2][:, 2 * c + g % 2, 2 * P * t : 2 * P * (t + 1)].bitcast(FP4X4),
                         lhsT_scale=es_sorted[part][:, c, g - es_spans[part][0], P * t : P * (t + 1)],
-                        rhs=xq_codes[:, c, qs].bitcast(FP8X4), rhs_scale=xq_scales[:, c, qs],
+                        rhs=xq_codes[i // 2][:, c, queries].bitcast(FP8X4), rhs_scale=xq_scales[i // 2][:, c, queries],
                         start=(c == 0), stop=(c == H_PASSES - 1),
                     )
             dst = z_early[g][:, i, :, :] if i < 2 else z_late[i][:, g, :, :]
             z = bank[:].rearrange("m t n -> m n t")
-            if on_vector:
+            if reader == VECTOR:
                 nc.vector.tensor_scalar(out=dst, in0=z, scalar1=0.0, scalar2=None, op0=ALU.max)
             else:
                 nc.scalar.activation(out=dst, in_=z, func=ACT.Relu)
 
-        units = [((g, 0), (g, 1)) for g in range(GROUPS)]
-        units = units + [((g, i), (g + 1, i)) for i in (2, 3) for g in range(0, GROUPS, 2)]
-
-        def log_z(u, b0, b1):
-            if b0 == 0:
-                z_log[u] = staged("z_log", [P, 2 * P, PACK], F32, 4)
-            g, i = units[u][0]
-            src = z_early[g] if i < 2 else z_late[i][:, g : g + 2, :, :]
+        def log_z(unit):
+            z_log[unit] = staged("z_log", [P, 2 * P, SLOTS], F32, 4)
+            g, i = unit[0]
+            src = z_early[g][:] if i < 2 else z_late[i][:, g : g + 2, :, :]
             nc.scalar.activation(
-                out=z_log[u][:, b0 * P : b1 * P, :].rearrange("m n t -> m (n t)"),
-                in_=src[:, b0:b1, :, :].rearrange("m b n t -> m (b n t)"),
+                out=z_log[unit][:].rearrange("m n t -> m (n t)"),
+                in_=src.rearrange("m b n t -> m (b n t)"),
                 func=ACT.Ln, bias=1.0,
             )
 
-        def weigh(u, b0, b1):
+        def weigh(unit, b0=0, b1=2):
             if b0 == 0:
-                u_t[u] = staged("u_t", [P, 2, P, PACK], BF16, 3)
-            g0, g1 = units[u][b0][0], units[u][b1 - 1][0]
-            factors = idf_cols[:, g0 : g1 + 1, :].unsqueeze(2).to_broadcast([P, b1 - b0, P, PACK])
-            logs = z_log[u][:, b0 * P : b1 * P, :].rearrange("m (b n) t -> m b n t", n=P)
-            nc.vector.tensor_tensor(out=u_t[u][:, b0:b1, :, :], in0=logs, in1=factors, op=ALU.mult)
+                u_t[unit] = staged("u_t", [P, 2, P, SLOTS], BF16, 3)
+            g0, g1 = unit[b0][0], unit[b1 - 1][0]
+            factors = idf_cols[:, g0 : g1 + 1, :].unsqueeze(2).to_broadcast([P, b1 - b0, P, SLOTS])
+            logs = z_log[unit][:, b0 * P : b1 * P, :].rearrange("m (b n) t -> m b n t", n=P)
+            nc.vector.tensor_tensor(out=u_t[unit][:, b0:b1, :, :], in0=logs, in1=factors, op=ALU.mult)
 
-        def quantize_u(u, b0, b1):
+        def quantize_u(unit, b0=0, b1=2):
             if b0 == 0:
-                u_codes[u] = staged("u_codes", [P, 2 * P], U32, 6)
-                u_scales[u] = staged("u_scales", [P, 2 * P], U8, 6)
+                u_codes[unit] = staged("u_codes", [P, 2 * P], U32, 6)
+                u_scales[unit] = staged("u_scales", [P, 2 * P], U8, 6)
             cols = slice(b0 * P, b1 * P)
-            quantize(u_codes[u][:, cols], u_scales[u][:, cols], u_t[u][:, b0:b1, :, :].rearrange("m b n t -> m (b n t)"))
+            values = u_t[unit][:, b0:b1, :, :].rearrange("m b n t -> m (b n t)")
+            quantize(u_codes[unit][:, cols], u_scales[unit][:, cols], values)
 
-        acc = {}
-        acc_bank = {(0, 0): 4, (0, 1): 5, (1, 0): 6, (1, 1): 7, (2, 0): 0, (2, 1): 1, (3, 0): 2, (3, 1): 3}
+        acc, acc_bank = {}, {}
 
-        def score(u, b, h):
-            g, i = units[u][b]
+        def score(unit, b, h):
+            g, i = unit[b]
             cols = slice(b * P, (b + 1) * P)
             docs = slice(h * HALF, (h + 1) * HALF)
             if g == 0:
                 acc[i, h] = take_bank(acc_bank[i, h], [P, HALF])
             nc.tensor.matmul_mx(
                 out=acc[i, h][:],
-                lhsT=u_codes[u][:, cols].bitcast(FP8X4), lhsT_scale=u_scales[u][:, cols],
+                lhsT=u_codes[unit][:, cols].bitcast(FP8X4), lhsT_scale=u_scales[unit][:, cols],
                 rhs=d_codes[g][:, docs].bitcast(FP8X4), rhs_scale=d_scales[g][:, docs],
                 start=(g == 0), stop=(g == GROUPS - 1),
             )
 
-        def score_tile(u, b):
+        def score_cell(unit, b):
             for h in range(HALVES):
-                score(u, b, h)
+                score(unit, b, h)
 
-        def store(i, h, on_vector):
+        def score_unit(unit):
+            for b in range(2):
+                score_cell(unit, b)
+
+        def store(i, h, reader):
             result = staged("result", [P, HALF], F32, 6)
-            copy_out(on_vector, result[:], acc[i, h][:])
+            copy_out(reader, result[:], acc[i, h][:])
             nc.sync.dma_start(out=out[i * P : (i + 1) * P, h * HALF : (h + 1) * HALF], in_=result[:])
 
-        warm_up(12)
+        warm_up(WARM_FIRST)
         sort_idf()
-        turn_xd(0, 0, False)
-        warm_up(8)
-        interleave_w(0, 0, 2)
-        load_w(2, 0, 1)
+        turn_xd(0, SCALAR)
+        turn_idf()
+        warm_up(WARM_SECOND)
         load_e_scales(0)
         load_e_words(0)
         load_e_scales(1)
-        interleave_w(0, 1, 2)
-        load_w(3, 0, 1)
+        interleave_w(0)
+        load_w(3)
         load_e_words(1)
-        quantize_xd(0, 0, 256)
+        quantize_xd(0)
         quantize_w(0)
-        turn_xd(0, 1, False)
-        turn_xd(1, 0, True)
-        warm_up(3)
-        quantize_xd(0, 256, 512)
+        turn_xd(1, SCALAR)
+        turn_xd(2, VECTOR)
+        warm_up(WARM_THIRD)
+        quantize_xd(1)
+        quantize_xd(2)
         make_d(0, 0)
         make_d(0, 1)
-        turn_xd(1, 1, False)
-        interleave_w(1, 0, 1)
-        load_w(4, 0, 1)
+        turn_xd(3, SCALAR)
+        interleave_w(1)
+        load_w(4)
         load_e_words(2)
         make_d(0, 2)
         make_d(0, 3)
-        quantize_xd(1, 0, 256)
+        quantize_xd(3)
         quantize_w(1)
-        quantize_xd(1, 256, 512)
-        turn_xq(0, 0, False)
-        make_d(0, 4, True)
-        make_d(0, 5)
-        turn_xq(1, 0, False)
-        interleave_w(2, 0, 1)
-        load_w(5, 0, 1)
+        make_d(0, 4)
+        make_d(0, 5, VECTOR)
+        turn_xq(0, 0, SCALAR)
+        turn_xq(0, 1, VECTOR)
         make_d(0, 6)
-        make_d(0, 7, True)
-        turn_xq(0, 1, False)
+        make_d(0, 7)
+        interleave_w(2)
+        load_w(5)
         make_d(1, 0)
         make_d(1, 1)
+        quantize_xq(0)
+        turn_xq(1, 0, VECTOR)
+        turn_xq(1, 1, SCALAR)
         sort_e_scales(0)
         sort_e_words(0)
-        turn_xq(1, 1, True)
-        turn_idf()
-        quantize_xq(0)
         make_d(1, 2)
         make_d(1, 3)
         quantize_xq(1)
-        quantize_d(0)
         make_d(1, 4)
         make_d(1, 5)
         make_d(1, 6)
-        banks[True] = (3,)
-        banks[False] = (0, 1, 2)
+        quantize_d(0)
 
-        for g in range(2, GROUPS):
-            u = g - 2
-            more = g + 1 < GROUPS
-            make_d(g - 1, 7, True)
+        by_age = [b for b in oldest_first if b != WARM_BANK]
+        banks_of[VECTOR] = by_age[0:1]
+        banks_of[SCALAR] = by_age[1:4]
+        for n, b in enumerate(by_age[4:] + [WARM_BANK] + by_age[1:4] + by_age[0:1]):
+            acc_bank[divmod(n, HALVES)] = b
+
+        for g in range(D_AHEAD, GROUPS):
+            u = g - D_AHEAD
+            has_scores = u >= 2
+            last_step = g == GROUPS - 1
+            make_d(g - 1, 7, VECTOR)
             quantize_w(g)
-            make_z(u, 0, False)
-            make_z(u, 1, False)
-            make_z(u, 2, False)
+            for i in range(3):
+                make_z(u, i, SCALAR)
             if u >= 1:
-                weigh(u - 1, 0, 2)
+                weigh(early[u - 1])
             else:
                 sort_e_scales(1)
-            if u < 2:
-                make_z(2 * u, 3, True)
+            if has_scores:
+                score_cell(early[u - 2], 0)
             else:
-                score_tile(u - 2, 0)
+                make_z(2 * u, 3, VECTOR)
             make_d(g, 0)
             quantize_d(g - 1)
             make_d(g, 1)
-            if u >= 2:
-                score(u - 2, 1, 0)
+            if has_scores:
+                score(early[u - 2], 1, 0)
             if u >= 1:
-                quantize_u(u - 1, 0, 2)
+                quantize_u(early[u - 1])
             make_d(g, 2)
-            if u < 2:
-                make_z(2 * u + 1, 3, True)
+            if has_scores:
+                make_d(g, 6, VECTOR)
             else:
-                make_d(g, 6, True)
+                make_z(2 * u + 1, 3, VECTOR)
             make_d(g, 3)
-            if u >= 2:
-                score(u - 2, 1, 1)
+            if has_scores:
+                score(early[u - 2], 1, 1)
             if u % 2 == 0:
                 sort_e_words(u // 2 + 1)
-            if more:
-                interleave_w(g + 1, 0, 1)
+            if last_step:
+                log_z(late[2][0])
             else:
-                log_z(GROUPS, 0, 2)
-            make_d(g, 4, not more, False)
-            make_d(g, 5, not more, False)
-            if u < 2:
-                make_d(g, 6, u == 1, False)
-            log_z(u, 0, 2)
+                interleave_w(g + 1)
+            make_d(g, 4, VECTOR if last_step else SCALAR, SCALAR)
+            make_d(g, 5, VECTOR if last_step else SCALAR, SCALAR)
+            if not has_scores:
+                make_d(g, 6, VECTOR if u == 1 else SCALAR, SCALAR)
+            log_z(early[u])
 
-        make_d(5, 7, True)
-        make_z(4, 0, False)
-        make_z(4, 1, False)
-        make_z(4, 2, False)
-        banks[False] = (2, 3)
-        banks[True] = (2, 3)
-        weigh(6, 0, 2)
-        weigh(3, 0, 2)
-        log_z(4, 0, 2)
-        make_z(5, 0, False)
-        score_tile(2, 0)
-        score_tile(2, 1)
-        make_z(5, 1, False)
-        quantize_u(6, 0, 2)
-        quantize_u(3, 0, 2)
-        quantize_d(5)
-        score_tile(3, 0)
-        score_tile(3, 1)
-        weigh(4, 0, 2)
-        make_z(5, 2, True)
-        log_z(7, 0, 2)
-        log_z(5, 0, 2)
-        make_z(4, 3, False)
-        score_tile(6, 0)
-        make_z(5, 3, False)
-        score_tile(6, 1)
-        weigh(7, 0, 2)
-        quantize_u(4, 0, 2)
-        score_tile(4, 0)
-        score_tile(4, 1)
-        log_z(8, 0, 2)
-        weigh(5, 0, 2)
-        quantize_u(7, 0, 2)
-        quantize_u(5, 0, 2)
-        score_tile(5, 0)
-        score_tile(5, 1)
-        score_tile(7, 0)
-        score_tile(7, 1)
-        log_z(9, 0, 2)
-        weigh(8, 0, 2)
-        log_z(10, 0, 2)
-        log_z(11, 0, 2)
-        halves = [(u, b) for u in (9, 10, 11) for b in range(2)]
-        weigh(9, 0, 1)
-        quantize_u(8, 0, 2)
-        score_tile(8, 0)
-        score_tile(8, 1)
-        for n in range(1, len(halves)):
-            weigh(halves[n][0], halves[n][1], halves[n][1] + 1)
-            quantize_u(halves[n - 1][0], halves[n - 1][1], halves[n - 1][1] + 1)
-            if n + 1 < len(halves):
-                score_tile(halves[n - 1][0], halves[n - 1][1])
+        make_d(GROUPS - 1, 7, VECTOR)
+        for i in range(3):
+            make_z(4, i, SCALAR)
+        banks_of[SCALAR] = (acc_bank[3, 0], acc_bank[3, 1])
+        banks_of[VECTOR] = banks_of[SCALAR]
+        weigh(late[2][0])
+        weigh(early[3])
+        log_z(early[4])
+        make_z(5, 0, SCALAR)
+        score_unit(early[2])
+        make_z(5, 1, SCALAR)
+        quantize_u(late[2][0])
+        quantize_u(early[3])
+        quantize_d(GROUPS - 1)
+        score_unit(early[3])
+        weigh(early[4])
+        make_z(5, 2, VECTOR)
+        log_z(late[2][1])
+        log_z(early[5])
+        make_z(4, 3, SCALAR)
+        score_cell(late[2][0], 0)
+        make_z(5, 3, SCALAR)
+        score_cell(late[2][0], 1)
+        weigh(late[2][1])
+        quantize_u(early[4])
+        score_unit(early[4])
+        log_z(late[2][2])
+        weigh(early[5])
+        quantize_u(late[2][1])
+        quantize_u(early[5])
+        score_unit(early[5])
+        score_unit(late[2][1])
+        log_z(late[3][0])
+        weigh(late[2][2])
+        log_z(late[3][1])
+        log_z(late[3][2])
+
+        cells = [(unit, b) for unit in late[3] for b in range(2)]
+        weigh(late[3][0], 0, 1)
+        quantize_u(late[2][2])
+        score_unit(late[2][2])
+        for n in range(1, len(cells)):
+            unit, b = cells[n]
+            unit_before, b_before = cells[n - 1]
+            weigh(unit, b, b + 1)
+            quantize_u(unit_before, b_before, b_before + 1)
+            if n + 1 < len(cells):
+                score_cell(unit_before, b_before)
         for i in range(3):
             for h in range(HALVES):
-                store(i, h, False)
-        quantize_u(11, 1, 2)
+                store(i, h, SCALAR)
+        quantize_u(late[3][2], 1, 2)
         for h in range(HALVES):
-            score(11, 0, h)
-            score(11, 1, h)
-            store(3, h, h == 0)
+            score(late[3][2], 0, h)
+            score(late[3][2], 1, h)
+            store(3, h, VECTOR if h == 0 else SCALAR)

@@ -26,11 +26,8 @@ BLOCKS = P // RUN
 HALF = 512
 HALVES = D // HALF
 PAIR = 2 * P
-PAIR_WORDS = K_PASS // 2
+PASS_WORDS = K_PASS // 2
 BANKS = 8
-WARM_BANK = BANKS - 1
-WARM_N = 256
-WARM_FIRST, WARM_SECOND, WARM_THIRD = 7, 6, 4
 D_AHEAD = 2
 SCALAR, VECTOR = False, True
 
@@ -50,15 +47,15 @@ def tile_log_saturated_latent_scoring_s11_kernel(tc, xq, e_words, e_scales, idf,
             return stage.tile(shape, dtype, name=tag, tag=tag, bufs=bufs, align_bytes=64)
 
         oldest_first = list(range(BANKS))
-        banks_of = {SCALAR: range(WARM_BANK), VECTOR: range(WARM_BANK)}
+        banks_of = {SCALAR: range(BANKS), VECTOR: range(BANKS)}
 
-        def take_bank(b, shape):
-            oldest_first.remove(b)
-            oldest_first.append(b)
-            return psum.tile(shape, F32, name="bank%d" % b, tag="bank%d" % b)
+        def take_bank(number, shape):
+            oldest_first.remove(number)
+            oldest_first.append(number)
+            return psum.tile(shape, F32, name="bank%d" % number, tag="bank%d" % number)
 
         def slot_bank(owner):
-            return take_bank([b for b in oldest_first if b in banks_of[owner]][0], [P, SLOTS, P])
+            return take_bank([number for number in oldest_first if number in banks_of[owner]][0], [P, SLOTS, P])
 
         def copy_out(reader, dst, src):
             if reader == VECTOR:
@@ -69,11 +66,6 @@ def tile_log_saturated_latent_scoring_s11_kernel(tc, xq, e_words, e_scales, idf,
         def quantize(codes, scales, values):
             nc.vector.quantize_mx(out=codes.bitcast(FP8X4), scales=scales, in_=values)
 
-        zeros = kept("zeros", [P, WARM_N * SLOTS], BF16)
-        nc.gpsimd.memset(zeros[:].bitcast(I32), 0)
-        zero_codes = kept("zero_codes", [P, WARM_N], U32)
-        zero_scales = kept("zero_scales", [P, WARM_N], U8)
-        quantize(zero_codes[:], zero_scales[:], zeros[:])
         ident = kept("ident", [P, P], F32)
         make_identity(nc, ident[:])
         idf_rows = kept("idf_rows", [P, K_PASS], F32)
@@ -99,11 +91,11 @@ def tile_log_saturated_latent_scoring_s11_kernel(tc, xq, e_words, e_scales, idf,
             xq_raw[i] = kept("xq_raw%d" % i, [P, H], BF16)
             nc.sync.dma_start(out=xq_raw[i][:], in_=xq[i * P : (i + 1) * P, :])
 
-        def load_e_words(n):
-            ew_raw[n] = kept("ew_raw%d" % n, [P, H_PASSES, K_PASS], I32)
+        def load_e_words(gg):
+            ew_raw[gg] = kept("ew_raw%d" % gg, [P, H_PASSES, K_PASS], I32)
             nc.sync.dma_start(
-                out=ew_raw[n][:],
-                in_=e_words.bitcast(I32)[:, :, n * K_PASS : (n + 1) * K_PASS].rearrange("c p v -> p c v"),
+                out=ew_raw[gg][:],
+                in_=e_words.bitcast(I32)[:, :, gg * K_PASS : (gg + 1) * K_PASS].rearrange("c p v -> p c v"),
             )
 
         def load_e_scales(part):
@@ -115,12 +107,12 @@ def tile_log_saturated_latent_scoring_s11_kernel(tc, xq, e_words, e_scales, idf,
                     in_=rows.bitcast(I32).rearrange("c r v -> r c v"),
                 )
 
-        idf_raw = kept("idf_raw", [GROUPS, K_PASS], BF16)
-        nc.scalar.dma_start(out=idf_raw[:], in_=idf.rearrange("(g v) -> g v", g=GROUPS))
         ln_table = kept("ln_table", [P, 1], F32)
-        nc.scalar.activation(out=ln_table[:], in_=zeros[:, 0:1], func=ACT.Ln, bias=1.0)
+        nc.scalar.activation(out=ln_table[:], in_=idf_rows[:, 0:1], func=ACT.Ln, bias=1.0)
 
         load_xd(0)
+        idf_raw = kept("idf_raw", [GROUPS, K_PASS], BF16)
+        nc.sync.dma_start(out=idf_raw[:], in_=idf.rearrange("(g v) -> g v", g=GROUPS))
         load_w(0)
         for pair in range(1, D // PAIR):
             load_xd(pair)
@@ -129,23 +121,13 @@ def tile_log_saturated_latent_scoring_s11_kernel(tc, xq, e_words, e_scales, idf,
             load_xq(i)
         load_w(2)
 
-        def warm_up(passes):
-            bank = take_bank(WARM_BANK, [P, WARM_N])
-            for n in range(passes):
-                nc.tensor.matmul_mx(
-                    out=bank[:],
-                    lhsT=zero_codes[:, 0:P].bitcast(FP8X4), lhsT_scale=zero_scales[:, 0:P],
-                    rhs=zero_codes[:].bitcast(FP8X4), rhs_scale=zero_scales[:],
-                    start=True, stop=True,
-                )
-
         xd_t = [kept("xd_t%d" % h, [P, HALF, SLOTS], BF16) for h in range(HALVES)]
         xd_codes = [kept("xd_codes%d" % h, [P, HALF], U32) for h in range(HALVES)]
         xd_scales = [kept("xd_scales%d" % h, [P, HALF], U8) for h in range(HALVES)]
 
         def pair_docs(pair):
-            h, n = divmod(pair, HALF // PAIR)
-            return h, slice(n * PAIR, (n + 1) * PAIR)
+            h, first = divmod(pair * PAIR, HALF)
+            return h, slice(first, first + PAIR)
 
         def turn_xd(pair, reader):
             h, docs = pair_docs(pair)
@@ -153,7 +135,7 @@ def tile_log_saturated_latent_scoring_s11_kernel(tc, xq, e_words, e_scales, idf,
             bank = slot_bank(reader)
             for a in range(2):
                 for odd in range(2):
-                    src = words[:, PAIR_WORDS * a + odd : PAIR_WORDS * (a + 1) : 2]
+                    src = words[:, PASS_WORDS * a + odd : PASS_WORDS * (a + 1) : 2]
                     nc.tensor.transpose(bank[:, 2 * a + odd, :], src, ident[:])
             dst = xd_t[h][:, docs, :].rearrange("k d t -> k (d t)").bitcast(F32)
             copy_out(reader, dst.rearrange("k (p j) -> k p j", j=4), bank[:].rearrange("k j p -> k p j"))
@@ -171,7 +153,7 @@ def tile_log_saturated_latent_scoring_s11_kernel(tc, xq, e_words, e_scales, idf,
             for a in range(2):
                 words = xq_raw[2 * pair + a][:].bitcast(F32)
                 for odd in range(2):
-                    src = words[:, PAIR_WORDS * c + odd : PAIR_WORDS * (c + 1) : 2]
+                    src = words[:, PASS_WORDS * c + odd : PASS_WORDS * (c + 1) : 2]
                     nc.tensor.transpose(bank[:, 2 * a + odd, :], src, ident[:])
             dst = xq_t[pair][:, c, :].bitcast(F32)
             copy_out(reader, dst.rearrange("k (a q o) -> k a q o", a=2, o=2), bank[:].rearrange("k (a o) q -> k a q o", o=2))
@@ -198,7 +180,7 @@ def tile_log_saturated_latent_scoring_s11_kernel(tc, xq, e_words, e_scales, idf,
             nc.scalar.copy(out=idf_cols[:], in_=bank[:, :, 0:GROUPS].rearrange("m t g -> m g t"))
 
         es_sorted = [kept("es_sorted%d" % g0, [P, H_PASSES, g1 - g0, K_PASS], U8) for g0, g1 in es_spans]
-        ew_sorted = [kept("ew_sorted%d" % n, [P, H_PASSES * 2, 2 * K_PASS], U8) for n in range(GROUPS // 2)]
+        ew_sorted = [kept("ew_sorted%d" % gg, [P, H_PASSES * 2, 2 * K_PASS], U8) for gg in range(GROUPS // 2)]
 
         def sort_e_scales(part):
             nc.vector.tensor_copy(
@@ -206,10 +188,10 @@ def tile_log_saturated_latent_scoring_s11_kernel(tc, xq, e_words, e_scales, idf,
                 in_=es_raw[part][:].bitcast(I32).rearrange("p c (g b t r) -> p (c g) t b r", t=SLOTS, b=BLOCKS, r=2),
             )
 
-        def sort_e_words(n):
+        def sort_e_words(gg):
             nc.vector.tensor_copy(
-                out=ew_sorted[n][:].bitcast(I32).rearrange("p s (t b r) -> p s t b r", t=SLOTS, b=BLOCKS),
-                in_=ew_raw[n][:].rearrange("p c (g b t r) -> p (c g) t b r", g=2, t=SLOTS, b=BLOCKS),
+                out=ew_sorted[gg][:].bitcast(I32).rearrange("p s (t b r) -> p s t b r", t=SLOTS, b=BLOCKS),
+                in_=ew_raw[gg][:].rearrange("p c (g b t r) -> p (c g) t b r", g=2, t=SLOTS, b=BLOCKS),
             )
 
         w_t, w_codes, w_scales = {}, {}, {}
@@ -255,7 +237,7 @@ def tile_log_saturated_latent_scoring_s11_kernel(tc, xq, e_words, e_scales, idf,
         z_early, z_log, u_t, u_codes, u_scales = {}, {}, {}, {}, {}
 
         def make_z(g, i, reader):
-            part = min(g // 2, 1)
+            part = 0 if g < es_spans[0][1] else 1
             if i == 0:
                 z_early[g] = staged("z_early", [P, 2, P, SLOTS], F32, 2)
             bank = slot_bank(reader)
@@ -282,31 +264,31 @@ def tile_log_saturated_latent_scoring_s11_kernel(tc, xq, e_words, e_scales, idf,
             src = z_early[g][:] if i < 2 else z_late[i][:, g : g + 2, :, :]
             nc.scalar.activation(
                 out=z_log[unit][:].rearrange("m n t -> m (n t)"),
-                in_=src.rearrange("m b n t -> m (b n t)"),
+                in_=src.rearrange("m e n t -> m (e n t)"),
                 func=ACT.Ln, bias=1.0,
             )
 
-        def weigh(unit, b0=0, b1=2):
-            if b0 == 0:
+        def weigh(unit, cell0=0, cell1=2):
+            if cell0 == 0:
                 u_t[unit] = staged("u_t", [P, 2, P, SLOTS], BF16, 3)
-            g0, g1 = unit[b0][0], unit[b1 - 1][0]
-            factors = idf_cols[:, g0 : g1 + 1, :].unsqueeze(2).to_broadcast([P, b1 - b0, P, SLOTS])
-            logs = z_log[unit][:, b0 * P : b1 * P, :].rearrange("m (b n) t -> m b n t", n=P)
-            nc.vector.tensor_tensor(out=u_t[unit][:, b0:b1, :, :], in0=logs, in1=factors, op=ALU.mult)
+            g0, g1 = unit[cell0][0], unit[cell1 - 1][0]
+            factors = idf_cols[:, g0 : g1 + 1, :].unsqueeze(2).to_broadcast([P, cell1 - cell0, P, SLOTS])
+            logs = z_log[unit][:, cell0 * P : cell1 * P, :].rearrange("m (e n) t -> m e n t", n=P)
+            nc.vector.tensor_tensor(out=u_t[unit][:, cell0:cell1, :, :], in0=logs, in1=factors, op=ALU.mult)
 
-        def quantize_u(unit, b0=0, b1=2):
-            if b0 == 0:
+        def quantize_u(unit, cell0=0, cell1=2):
+            if cell0 == 0:
                 u_codes[unit] = staged("u_codes", [P, 2 * P], U32, 6)
                 u_scales[unit] = staged("u_scales", [P, 2 * P], U8, 6)
-            cols = slice(b0 * P, b1 * P)
-            values = u_t[unit][:, b0:b1, :, :].rearrange("m b n t -> m (b n t)")
+            cols = slice(cell0 * P, cell1 * P)
+            values = u_t[unit][:, cell0:cell1, :, :].rearrange("m e n t -> m (e n t)")
             quantize(u_codes[unit][:, cols], u_scales[unit][:, cols], values)
 
         acc, acc_bank = {}, {}
 
-        def score(unit, b, h):
-            g, i = unit[b]
-            cols = slice(b * P, (b + 1) * P)
+        def score(unit, cell, h):
+            g, i = unit[cell]
+            cols = slice(cell * P, (cell + 1) * P)
             docs = slice(h * HALF, (h + 1) * HALF)
             if g == 0:
                 acc[i, h] = take_bank(acc_bank[i, h], [P, HALF])
@@ -317,24 +299,22 @@ def tile_log_saturated_latent_scoring_s11_kernel(tc, xq, e_words, e_scales, idf,
                 start=(g == 0), stop=(g == GROUPS - 1),
             )
 
-        def score_cell(unit, b):
+        def score_cell(unit, cell):
             for h in range(HALVES):
-                score(unit, b, h)
+                score(unit, cell, h)
 
         def score_unit(unit):
-            for b in range(2):
-                score_cell(unit, b)
+            for cell in range(2):
+                score_cell(unit, cell)
 
         def store(i, h, reader):
             result = staged("result", [P, HALF], F32, 6)
             copy_out(reader, result[:], acc[i, h][:])
             nc.sync.dma_start(out=out[i * P : (i + 1) * P, h * HALF : (h + 1) * HALF], in_=result[:])
 
-        warm_up(WARM_FIRST)
         sort_idf()
         turn_xd(0, SCALAR)
         turn_idf()
-        warm_up(WARM_SECOND)
         load_e_scales(0)
         load_e_words(0)
         load_e_scales(1)
@@ -344,34 +324,31 @@ def tile_log_saturated_latent_scoring_s11_kernel(tc, xq, e_words, e_scales, idf,
         quantize_xd(0)
         quantize_w(0)
         turn_xd(1, SCALAR)
-        turn_xd(2, VECTOR)
-        warm_up(WARM_THIRD)
+        turn_xd(2, SCALAR)
         quantize_xd(1)
-        quantize_xd(2)
-        make_d(0, 0)
-        make_d(0, 1)
-        turn_xd(3, SCALAR)
         interleave_w(1)
         load_w(4)
         load_e_words(2)
-        make_d(0, 2)
-        make_d(0, 3)
-        quantize_xd(3)
+        quantize_xd(2)
         quantize_w(1)
+        for n in range(4):
+            make_d(0, n)
+        turn_xd(3, VECTOR)
         make_d(0, 4)
         make_d(0, 5, VECTOR)
+        quantize_xd(3)
         turn_xq(0, 0, SCALAR)
         turn_xq(0, 1, VECTOR)
-        make_d(0, 6)
-        make_d(0, 7)
         interleave_w(2)
         load_w(5)
         make_d(1, 0)
         make_d(1, 1)
+        make_d(0, 6)
+        make_d(0, 7)
         quantize_xq(0)
+        sort_e_scales(0)
         turn_xq(1, 0, VECTOR)
         turn_xq(1, 1, SCALAR)
-        sort_e_scales(0)
         sort_e_words(0)
         make_d(1, 2)
         make_d(1, 3)
@@ -381,11 +358,12 @@ def tile_log_saturated_latent_scoring_s11_kernel(tc, xq, e_words, e_scales, idf,
         make_d(1, 6)
         quantize_d(0)
 
-        by_age = [b for b in oldest_first if b != WARM_BANK]
+        by_age = list(oldest_first)
         banks_of[VECTOR] = by_age[0:1]
         banks_of[SCALAR] = by_age[1:4]
-        for n, b in enumerate(by_age[4:] + [WARM_BANK] + by_age[1:4] + by_age[0:1]):
-            acc_bank[divmod(n, HALVES)] = b
+        outputs = [(i, h) for i in range(Q // P) for h in range(HALVES)]
+        for output, number in zip(outputs, by_age[4:] + by_age[1:4] + by_age[0:1]):
+            acc_bank[output] = number
 
         for g in range(D_AHEAD, GROUPS):
             u = g - D_AHEAD
@@ -467,17 +445,15 @@ def tile_log_saturated_latent_scoring_s11_kernel(tc, xq, e_words, e_scales, idf,
         log_z(late[3][1])
         log_z(late[3][2])
 
-        cells = [(unit, b) for unit in late[3] for b in range(2)]
+        cells = [(unit, cell) for unit in late[3] for cell in range(2)]
         weigh(late[3][0], 0, 1)
         quantize_u(late[2][2])
         score_unit(late[2][2])
-        for n in range(1, len(cells)):
-            unit, b = cells[n]
-            unit_before, b_before = cells[n - 1]
-            weigh(unit, b, b + 1)
-            quantize_u(unit_before, b_before, b_before + 1)
-            if n + 1 < len(cells):
-                score_cell(unit_before, b_before)
+        for (unit_before, cell_before), (unit, cell) in zip(cells, cells[1:]):
+            weigh(unit, cell, cell + 1)
+            quantize_u(unit_before, cell_before, cell_before + 1)
+            if (unit, cell) != cells[-1]:
+                score_cell(unit_before, cell_before)
         for i in range(3):
             for h in range(HALVES):
                 store(i, h, SCALAR)

from contextlib import ExitStack

import concourse.mybir as mybir
from concourse.masks import make_identity

Q, H, V, D, L = 512, 1024, 3072, 1024, 512
FLOPS = 2 * Q * H * V + 2 * D * L * V + 2 * Q * V * D

F32 = mybir.dt.float32
BF16 = mybir.dt.bfloat16
I32 = mybir.dt.int32
U32 = mybir.dt.uint32
U8 = mybir.dt.uint8
FP8X4 = mybir.dt.float8_e4m3fn_x4
FP4X4 = mybir.dt.float4_e2m1fn_x4
ALU = mybir.AluOpType
ACT = mybir.ActivationFunctionType

P = 128
SLOTS = 4
K_PASS = P * SLOTS
GROUPS = V // K_PASS
H_PASSES = H // K_PASS
RUN = 8
BLOCKS = P // RUN
HALF = 512
HALVES = D // HALF
PAIR = 2 * P
PASS_WORDS = K_PASS // 2
BANKS = 8
D_AHEAD = 2
SCALAR, VECTOR = False, True


def tile_log_saturated_latent_scoring_s11_kernel(tc, xq, e_words, e_scales, idf, xd, w, out):
    nc = tc.nc
    with ExitStack() as ctx:
        keep = ctx.enter_context(tc.tile_pool(name="keep", bufs=1))
        stage = ctx.enter_context(tc.tile_pool(name="stage", bufs=2))
        psum = ctx.enter_context(tc.psum_pool(name="psum", bufs=1))
        ctx.enter_context(tc.manual_schedule())

        def kept(name, shape, dtype):
            return keep.tile(shape, dtype, name=name, align_bytes=64)

        def staged(tag, shape, dtype, bufs):
            return stage.tile(shape, dtype, name=tag, tag=tag, bufs=bufs, align_bytes=64)

        oldest_first = list(range(BANKS))
        banks_of = {SCALAR: range(BANKS), VECTOR: range(BANKS)}

        def take_bank(number, shape):
            oldest_first.remove(number)
            oldest_first.append(number)
            return psum.tile(shape, F32, name="bank%d" % number, tag="bank%d" % number)

        def slot_bank(owner):
            return take_bank([number for number in oldest_first if number in banks_of[owner]][0], [P, SLOTS, P])

        def copy_out(reader, dst, src):
            if reader == VECTOR:
                nc.vector.tensor_copy(out=dst, in_=src)
            else:
                nc.scalar.copy(out=dst, in_=src)

        def quantize(codes, scales, values):
            nc.vector.quantize_mx(out=codes.bitcast(FP8X4), scales=scales, in_=values)

        ident = kept("ident", [P, P], F32)
        make_identity(nc, ident[:])
        idf_rows = kept("idf_rows", [P, K_PASS], F32)
        nc.vector.memset(idf_rows[:], 0.0)
        es_spans = ((0, 2), (2, GROUPS))
        es_raw = [kept("es_raw%d" % g0, [P, H_PASSES, (g1 - g0) * K_PASS], U8) for g0, g1 in es_spans]
        for raw in es_raw:
            nc.vector.memset(raw[:].bitcast(I32), 0)

        xd_raw, w_raw, xq_raw, ew_raw = {}, {}, {}, {}

        def load_xd(pair):
            xd_raw[pair] = kept("xd_raw%d" % pair, [P, 2 * L], BF16)
            rows = xd[pair * PAIR : (pair + 1) * PAIR, :]
            nc.sync.dma_start(out=xd_raw[pair][:], in_=rows.rearrange("(p a) k -> p (a k)", a=2))

        def load_w(g):
            w_raw[g] = staged("w_raw", [P, SLOTS, K_PASS], BF16, 3)
            cols = w[:, g * K_PASS : (g + 1) * K_PASS]
            nc.sync.dma_start(out=w_raw[g][:], in_=cols.rearrange("(p j) v -> p j v", j=SLOTS))

        def load_xq(i):
            xq_raw[i] = kept("xq_raw%d" % i, [P, H], BF16)
            nc.sync.dma_start(out=xq_raw[i][:], in_=xq[i * P : (i + 1) * P, :])

        def load_e_words(gg):
            ew_raw[gg] = kept("ew_raw%d" % gg, [P, H_PASSES, K_PASS], I32)
            nc.sync.dma_start(
                out=ew_raw[gg][:],
                in_=e_words.bitcast(I32)[:, :, gg * K_PASS : (gg + 1) * K_PASS].rearrange("c p v -> p c v"),
            )

        def load_e_scales(part):
            g0, g1 = es_spans[part]
            for j in range(4):
                rows = e_scales[:, 4 * j : 4 * j + 4, g0 * K_PASS : g1 * K_PASS]
                nc.sync.dma_start(
                    out=es_raw[part][32 * j : 32 * j + 4, :, :].bitcast(I32),
                    in_=rows.bitcast(I32).rearrange("c r v -> r c v"),
                )

        ln_table = kept("ln_table", [P, 1], F32)
        nc.scalar.activation(out=ln_table[:], in_=idf_rows[:, 0:1], func=ACT.Ln, bias=1.0)

        load_xd(0)
        idf_raw = kept("idf_raw", [GROUPS, K_PASS], BF16)
        nc.sync.dma_start(out=idf_raw[:], in_=idf.rearrange("(g v) -> g v", g=GROUPS))
        load_w(0)
        for pair in range(1, D // PAIR):
            load_xd(pair)
        load_w(1)
        for i in range(Q // P):
            load_xq(i)
        load_w(2)

        xd_t = [kept("xd_t%d" % h, [P, HALF, SLOTS], BF16) for h in range(HALVES)]
        xd_codes = [kept("xd_codes%d" % h, [P, HALF], U32) for h in range(HALVES)]
        xd_scales = [kept("xd_scales%d" % h, [P, HALF], U8) for h in range(HALVES)]

        def pair_docs(pair):
            h, first = divmod(pair * PAIR, HALF)
            return h, slice(first, first + PAIR)

        def turn_xd(pair, reader):
            h, docs = pair_docs(pair)
            words = xd_raw[pair][:].bitcast(F32)
            bank = slot_bank(reader)
            for a in range(2):
                for odd in range(2):
                    src = words[:, PASS_WORDS * a + odd : PASS_WORDS * (a + 1) : 2]
                    nc.tensor.transpose(bank[:, 2 * a + odd, :], src, ident[:])
            dst = xd_t[h][:, docs, :].rearrange("k d t -> k (d t)").bitcast(F32)
            copy_out(reader, dst.rearrange("k (p j) -> k p j", j=4), bank[:].rearrange("k j p -> k p j"))

        def quantize_xd(pair):
            h, docs = pair_docs(pair)
            quantize(xd_codes[h][:, docs], xd_scales[h][:, docs], xd_t[h][:, docs, :].rearrange("k d t -> k (d t)"))

        xq_t = [kept("xq_t%d" % pair, [P, H_PASSES, PAIR * SLOTS], BF16) for pair in range(Q // PAIR)]
        xq_codes = [kept("xq_codes%d" % pair, [P, H_PASSES, PAIR], U32) for pair in range(Q // PAIR)]
        xq_scales = [kept("xq_scales%d" % pair, [P, H_PASSES, PAIR], U8) for pair in range(Q // PAIR)]

        def turn_xq(pair, c, reader):
            bank = slot_bank(reader)
            for a in range(2):
                words = xq_raw[2 * pair + a][:].bitcast(F32)
                for odd in range(2):
                    src = words[:, PASS_WORDS * c + odd : PASS_WORDS * (c + 1) : 2]
                    nc.tensor.transpose(bank[:, 2 * a + odd, :], src, ident[:])
            dst = xq_t[pair][:, c, :].bitcast(F32)
            copy_out(reader, dst.rearrange("k (a q o) -> k a q o", a=2, o=2), bank[:].rearrange("k (a o) q -> k a q o", o=2))

        def quantize_xq(pair):
            quantize(
                xq_codes[pair][:].rearrange("k c q -> k (c q)"),
                xq_scales[pair][:].rearrange("k c q -> k (c q)"),
                xq_t[pair][:].rearrange("k c n -> k (c n)"),
            )

        idf_cols = kept("idf_cols", [P, GROUPS, SLOTS], F32)

        def sort_idf():
            nc.scalar.copy(
                out=idf_rows[0:GROUPS, :].rearrange("g (t b r) -> g t b r", t=SLOTS, r=RUN),
                in_=idf_raw[:].rearrange("g (b t r) -> g t b r", t=SLOTS, r=RUN),
            )

        def turn_idf():
            bank = slot_bank(SCALAR)
            for t in range(SLOTS):
                nc.tensor.transpose(bank[:, t, :], idf_rows[:, t * P : (t + 1) * P], ident[:])
            nc.scalar.copy(out=idf_cols[:], in_=bank[:, :, 0:GROUPS].rearrange("m t g -> m g t"))

        es_sorted = [kept("es_sorted%d" % g0, [P, H_PASSES, g1 - g0, K_PASS], U8) for g0, g1 in es_spans]
        ew_sorted = [kept("ew_sorted%d" % gg, [P, H_PASSES * 2, 2 * K_PASS], U8) for gg in range(GROUPS // 2)]

        def sort_e_scales(part):
            nc.vector.tensor_copy(
                out=es_sorted[part][:].bitcast(I32).rearrange("p c g (t b r) -> p (c g) t b r", t=SLOTS, b=BLOCKS),
                in_=es_raw[part][:].bitcast(I32).rearrange("p c (g b t r) -> p (c g) t b r", t=SLOTS, b=BLOCKS, r=2),
            )

        def sort_e_words(gg):
            nc.vector.tensor_copy(
                out=ew_sorted[gg][:].bitcast(I32).rearrange("p s (t b r) -> p s t b r", t=SLOTS, b=BLOCKS),
                in_=ew_raw[gg][:].rearrange("p c (g b t r) -> p (c g) t b r", g=2, t=SLOTS, b=BLOCKS),
            )

        w_t, w_codes, w_scales = {}, {}, {}

        def interleave_w(g):
            w_t[g] = staged("w_t", [P, K_PASS * SLOTS], BF16, 2)
            nc.vector.tensor_copy(
                out=w_t[g][:].rearrange("p (t b r j) -> p t b r j", t=SLOTS, r=RUN, j=SLOTS),
                in_=w_raw[g][:].rearrange("p j (b t r) -> p t b r j", t=SLOTS, r=RUN),
            )

        def quantize_w(g):
            w_codes[g] = staged("w_codes", [P, K_PASS], U32, 2)
            w_scales[g] = staged("w_scales", [P, K_PASS], U8, 2)
            quantize(w_codes[g][:], w_scales[g][:], w_t[g][:])

        d_t, d_codes, d_scales = {}, {}, {}

        def make_d(g, n, reader=SCALAR, owner=None):
            h, first = divmod(n * P, HALF)
            if g not in d_t:
                d_t[g] = staged("d_t", [P, D, SLOTS], BF16, 2)
            docs = slice(first, first + P)
            bank = slot_bank(reader if owner is None else owner)
            for t in range(SLOTS):
                terms = slice(t * P, (t + 1) * P)
                nc.tensor.matmul_mx(
                    out=bank[:, t, :],
                    lhsT=w_codes[g][:, terms].bitcast(FP8X4), lhsT_scale=w_scales[g][:, terms],
                    rhs=xd_codes[h][:, docs].bitcast(FP8X4), rhs_scale=xd_scales[h][:, docs],
                    start=True, stop=True,
                )
            copy_out(reader, d_t[g][:, n * P : (n + 1) * P, :], bank[:].rearrange("m t n -> m n t"))

        def quantize_d(g):
            d_codes[g] = kept("d_codes%d" % g, [P, D], U32)
            d_scales[g] = kept("d_scales%d" % g, [P, D], U8)
            quantize(d_codes[g][:], d_scales[g][:], d_t[g][:].rearrange("m n t -> m (n t)"))

        early = [((g, 0), (g, 1)) for g in range(GROUPS)]
        late = {i: [((g, i), (g + 1, i)) for g in range(0, GROUPS, 2)] for i in (2, 3)}
        z_late = {i: kept("z_late%d" % i, [P, GROUPS, P, SLOTS], F32) for i in (2, 3)}
        z_early, z_log, u_t, u_codes, u_scales = {}, {}, {}, {}, {}

        def make_z(g, i, reader):
            part = 0 if g < es_spans[0][1] else 1
            if i == 0:
                z_early[g] = staged("z_early", [P, 2, P, SLOTS], F32, 2)
            bank = slot_bank(reader)
            queries = slice(i % 2 * P, (i % 2 + 1) * P)
            for t in range(SLOTS):
                for c in range(H_PASSES):
                    nc.tensor.matmul_mx(
                        out=bank[:, t, :],
                        lhsT=ew_sorted[g // 2][:, 2 * c + g % 2, 2 * P * t : 2 * P * (t + 1)].bitcast(FP4X4),
                        lhsT_scale=es_sorted[part][:, c, g - es_spans[part][0], P * t : P * (t + 1)],
                        rhs=xq_codes[i // 2][:, c, queries].bitcast(FP8X4), rhs_scale=xq_scales[i // 2][:, c, queries],
                        start=(c == 0), stop=(c == H_PASSES - 1),
                    )
            dst = z_early[g][:, i, :, :] if i < 2 else z_late[i][:, g, :, :]
            z = bank[:].rearrange("m t n -> m n t")
            if reader == VECTOR:
                nc.vector.tensor_scalar(out=dst, in0=z, scalar1=0.0, scalar2=None, op0=ALU.max)
            else:
                nc.scalar.activation(out=dst, in_=z, func=ACT.Relu)

        def log_z(unit):
            z_log[unit] = staged("z_log", [P, 2 * P, SLOTS], F32, 4)
            g, i = unit[0]
            src = z_early[g][:] if i < 2 else z_late[i][:, g : g + 2, :, :]
            nc.scalar.activation(
                out=z_log[unit][:].rearrange("m n t -> m (n t)"),
                in_=src.rearrange("m e n t -> m (e n t)"),
                func=ACT.Ln, bias=1.0,
            )

        def weigh(unit, cell0=0, cell1=2):
            if cell0 == 0:
                u_t[unit] = staged("u_t", [P, 2, P, SLOTS], BF16, 3)
            g0, g1 = unit[cell0][0], unit[cell1 - 1][0]
            factors = idf_cols[:, g0 : g1 + 1, :].unsqueeze(2).to_broadcast([P, cell1 - cell0, P, SLOTS])
            logs = z_log[unit][:, cell0 * P : cell1 * P, :].rearrange("m (e n) t -> m e n t", n=P)
            nc.vector.tensor_tensor(out=u_t[unit][:, cell0:cell1, :, :], in0=logs, in1=factors, op=ALU.mult)

        def quantize_u(unit, cell0=0, cell1=2):
            if cell0 == 0:
                u_codes[unit] = staged("u_codes", [P, 2 * P], U32, 6)
                u_scales[unit] = staged("u_scales", [P, 2 * P], U8, 6)
            cols = slice(cell0 * P, cell1 * P)
            values = u_t[unit][:, cell0:cell1, :, :].rearrange("m e n t -> m (e n t)")
            quantize(u_codes[unit][:, cols], u_scales[unit][:, cols], values)

        acc, acc_bank = {}, {}

        def score(unit, cell, h):
            g, i = unit[cell]
            cols = slice(cell * P, (cell + 1) * P)
            docs = slice(h * HALF, (h + 1) * HALF)
            if g == 0:
                acc[i, h] = take_bank(acc_bank[i, h], [P, HALF])
            nc.tensor.matmul_mx(
                out=acc[i, h][:],
                lhsT=u_codes[unit][:, cols].bitcast(FP8X4), lhsT_scale=u_scales[unit][:, cols],
                rhs=d_codes[g][:, docs].bitcast(FP8X4), rhs_scale=d_scales[g][:, docs],
                start=(g == 0), stop=(g == GROUPS - 1),
            )

        def score_cell(unit, cell):
            for h in range(HALVES):
                score(unit, cell, h)

        def score_unit(unit):
            for cell in range(2):
                score_cell(unit, cell)

        def store(i, h, reader):
            result = staged("result", [P, HALF], F32, 6)
            copy_out(reader, result[:], acc[i, h][:])
            nc.sync.dma_start(out=out[i * P : (i + 1) * P, h * HALF : (h + 1) * HALF], in_=result[:])

        sort_idf()
        turn_xd(0, SCALAR)
        turn_idf()
        load_e_scales(0)
        load_e_words(0)
        load_e_scales(1)
        interleave_w(0)
        load_w(3)
        load_e_words(1)
        quantize_xd(0)
        quantize_w(0)
        turn_xd(1, SCALAR)
        turn_xd(2, SCALAR)
        quantize_xd(1)
        interleave_w(1)
        load_w(4)
        load_e_words(2)
        quantize_xd(2)
        quantize_w(1)
        for n in range(4):
            make_d(0, n)
        turn_xd(3, VECTOR)
        make_d(0, 4)
        make_d(0, 5, VECTOR)
        quantize_xd(3)
        turn_xq(0, 0, SCALAR)
        turn_xq(0, 1, VECTOR)
        interleave_w(2)
        load_w(5)
        make_d(1, 0)
        make_d(1, 1)
        make_d(0, 6)
        make_d(0, 7)
        quantize_xq(0)
        sort_e_scales(0)
        turn_xq(1, 0, VECTOR)
        turn_xq(1, 1, SCALAR)
        sort_e_words(0)
        make_d(1, 2)
        make_d(1, 3)
        quantize_xq(1)
        make_d(1, 4)
        make_d(1, 5)
        make_d(1, 6)
        quantize_d(0)

        by_age = list(oldest_first)
        banks_of[VECTOR] = by_age[0:1]
        banks_of[SCALAR] = by_age[1:4]
        outputs = [(i, h) for i in range(Q // P) for h in range(HALVES)]
        for output, number in zip(outputs, by_age[4:] + by_age[1:4] + by_age[0:1]):
            acc_bank[output] = number

        for g in range(D_AHEAD, GROUPS):
            u = g - D_AHEAD
            has_scores = u >= 2
            last_step = g == GROUPS - 1
            make_d(g - 1, 7, VECTOR)
            quantize_w(g)
            for i in range(3):
                make_z(u, i, SCALAR)
            if u >= 1:
                weigh(early[u - 1])
            else:
                sort_e_scales(1)
            if has_scores:
                score_cell(early[u - 2], 0)
            else:
                make_z(2 * u, 3, VECTOR)
            make_d(g, 0)
            quantize_d(g - 1)
            make_d(g, 1)
            if has_scores:
                score(early[u - 2], 1, 0)
            if u >= 1:
                quantize_u(early[u - 1])
            make_d(g, 2)
            if has_scores:
                make_d(g, 6, VECTOR)
            else:
                make_z(2 * u + 1, 3, VECTOR)
            make_d(g, 3)
            if has_scores:
                score(early[u - 2], 1, 1)
            if u % 2 == 0:
                sort_e_words(u // 2 + 1)
            if last_step:
                log_z(late[2][0])
            else:
                interleave_w(g + 1)
            make_d(g, 4, VECTOR if last_step else SCALAR, SCALAR)
            make_d(g, 5, VECTOR if last_step else SCALAR, SCALAR)
            if not has_scores:
                make_d(g, 6, VECTOR if u == 1 else SCALAR, SCALAR)
            log_z(early[u])

        make_d(GROUPS - 1, 7, VECTOR)
        for i in range(3):
            make_z(4, i, SCALAR)
        banks_of[SCALAR] = (acc_bank[3, 0], acc_bank[3, 1])
        banks_of[VECTOR] = banks_of[SCALAR]
        weigh(late[2][0])
        weigh(early[3])
        log_z(early[4])
        make_z(5, 0, SCALAR)
        score_unit(early[2])
        make_z(5, 1, SCALAR)
        quantize_u(late[2][0])
        quantize_u(early[3])
        quantize_d(GROUPS - 1)
        score_unit(early[3])
        weigh(early[4])
        make_z(5, 2, VECTOR)
        log_z(late[2][1])
        log_z(early[5])
        make_z(4, 3, SCALAR)
        score_cell(late[2][0], 0)
        make_z(5, 3, SCALAR)
        score_cell(late[2][0], 1)
        weigh(late[2][1])
        quantize_u(early[4])
        score_unit(early[4])
        log_z(late[2][2])
        weigh(early[5])
        quantize_u(late[2][1])
        quantize_u(early[5])
        score_unit(early[5])
        score_unit(late[2][1])
        log_z(late[3][0])
        weigh(late[2][2])
        log_z(late[3][1])
        log_z(late[3][2])

        cells = [(unit, cell) for unit in late[3] for cell in range(2)]
        weigh(late[3][0], 0, 1)
        quantize_u(late[2][2])
        score_unit(late[2][2])
        for (unit_before, cell_before), (unit, cell) in zip(cells, cells[1:]):
            weigh(unit, cell, cell + 1)
            quantize_u(unit_before, cell_before, cell_before + 1)
            if (unit, cell) != cells[-1]:
                score_cell(unit_before, cell_before)
        for i in range(3):
            for h in range(HALVES):
                store(i, h, SCALAR)
        quantize_u(late[3][2], 1, 2)
        for h in range(HALVES):
            score(late[3][2], 0, h)
            score(late[3][2], 1, h)
            store(3, h, VECTOR if h == 0 else SCALAR)
